import numpy as np
import ml_dtypes


def mxq(x, axis, fmt="e4m3"):
    dtype, down = {"e4m3": (ml_dtypes.float8_e4m3fn, 7), "e5m2": (ml_dtypes.float8_e5m2, 14)}[fmt]
    v = np.moveaxis(np.asarray(x, np.float32).astype(ml_dtypes.bfloat16).astype(np.float64), axis, -1)
    blocks = v.reshape(v.shape[:-1] + (-1, 32))
    amax = np.abs(blocks).max(-1, keepdims=True)
    byte = np.maximum(np.where(amax > 0, np.frexp(amax)[1] - 1 + 127, 0) - down, 1)
    scale = np.exp2(byte - 127.0)
    codes = (blocks / scale).astype(np.float32).astype(dtype).astype(np.float64)
    return np.moveaxis((codes * scale).reshape(v.shape), -1, axis)


WIDE = False


def mx_kscale(k):
    if not WIDE:
        return np.ones(k)
    levels = np.array([10, -10, 5, -5, 0])
    if k % 512:
        return np.exp2(np.random.permutation(np.resize(levels, k // 32))).repeat(32)
    a = np.empty((k // 512, 16))
    for p in range(k // 512):
        a[p, :8] = np.random.permutation(np.resize(levels, 8))
        for g in range(8):
            far = levels[np.abs(levels - a[p, g]) >= 10]
            a[p, g + 8] = far[np.random.randint(len(far))]
    return np.exp2(a.ravel()).repeat(32)


BF16 = ml_dtypes.bfloat16


def bf(x):
    return np.asarray(x, np.float32).astype(BF16)


def f64(x):
    return np.asarray(x).astype(np.float64)


E2M1 = np.array([0.0, 0.5, 1.0, 1.5, 2.0, 3.0, 4.0, 6.0, -0.0, -0.5, -1.0, -1.5, -2.0, -3.0, -4.0, -6.0])


def pack_weight(w, fmt):
    k, n = w.shape
    w = f64(bf(w)).reshape(k // 32, 32, n)
    amax = np.abs(w).max(1)
    if fmt == "e4m3":
        byte = np.frexp(amax)[1] - 1 + 127 - 7
    else:
        mant, ex = np.frexp(amax / 6.0)
        byte = np.where(mant > 0.5, ex, ex - 1) + 127
    byte = np.clip(np.where(amax > 0, byte, 1), 1, 254)
    scaled = (w * np.exp2(127.0 - byte)[:, None, :]).reshape(k, n).astype(np.float32)
    by_word = np.ascontiguousarray(scaled.reshape(k // 512, 128, 4, n).transpose(0, 1, 3, 2))
    if fmt == "e4m3":
        words = by_word.astype(ml_dtypes.float8_e4m3fn).view(np.uint8)
    else:
        c = by_word.astype(ml_dtypes.float4_e2m1fn).view(np.uint8) & 0xF
        words = c[..., 0::2] | (c[..., 1::2] << 4)
    return np.ascontiguousarray(words), np.ascontiguousarray(byte.astype(np.uint8).reshape(k // 512, 16, n))


def unpack_weight(words, scales, fmt):
    g, p, n, _ = words.shape
    if fmt == "e4m3":
        vals = np.ascontiguousarray(words).view(ml_dtypes.float8_e4m3fn).astype(np.float64)
    else:
        nib = np.empty((g, p, n, 4), np.uint8)
        nib[..., 0::2] = words & 0xF
        nib[..., 1::2] = words >> 4
        vals = E2M1[nib]
    vals = vals * np.repeat(np.exp2(scales.astype(np.float64) - 127.0), 8, axis=1)[..., None]
    return vals.transpose(0, 1, 3, 2).reshape(g * 512, n)
def pack4(w):
    words, scales = pack_weight(w, "e2m1")
    return words.reshape(words.shape[0], 128, -1), scales


def unpack4(words, scales):
    return unpack_weight(words.reshape(words.shape[0], 128, -1, 2), scales, "e2m1")


B, E, D, S = 1024, 1024, 512, 2048


def setup_inputs():
    s, u, t = mx_kscale(E), mx_kscale(D), mx_kscale(S)
    counts = np.random.randint(-3, 4, (E, S)).astype(np.float64)
    mass = np.random.uniform(0.5, 1.5, E)
    f_words, f_scales = pack4(counts / (2 * np.sqrt(E)) / s[:, None])
    a_words, a_scales = pack4(counts.T * mass / (2 * np.sqrt(S)) / t[:, None])
    return {"lam": bf(0.6 * np.random.standard_normal((B, E)) * s),
            "f_words": f_words, "f_scales": f_scales,
            "phi": bf(0.5 * np.random.standard_normal((B, D)) * u),
            "g": bf(np.random.standard_normal((D, S)) / np.sqrt(D) / u[:, None]),
            "m": bf(np.random.uniform(0.5, 1.5, S) * t),
            "a_words": a_words, "a_scales": a_scales,
            "feed": bf(np.random.standard_normal((B, E)))}


def reference(lam, f_words, f_scales, phi, g, m, a_words, a_scales, feed):
    F = unpack4(f_words, f_scales)
    A = unpack4(a_words, a_scales)
    z = (mxq(f64(lam), 1, "e4m3") @ F) + (mxq(f64(phi), 1, "e4m3") @ mxq(f64(g), 0, "e4m3"))
    n = np.exp(z) * f64(m)
    return (mxq(n, 1, "e4m3") @ A) - f64(feed)

@@ -1,0 +1,277 @@
+from contextlib import ExitStack
+
+import concourse.mybir as mybir
+from concourse.masks import make_identity
+
+B, E, D, S = 1024, 1024, 512, 2048
+FLOPS = 2 * B * S * (E + D) + 2 * B * E * S
+
+F32 = mybir.dt.float32
+BF16 = mybir.dt.bfloat16
+I32 = mybir.dt.int32
+U32 = mybir.dt.uint32
+U8 = mybir.dt.uint8
+FP8X4 = mybir.dt.float8_e4m3fn_x4
+FP4X4 = mybir.dt.float4_e2m1fn_x4
+ALU = mybir.AluOpType
+ACT = mybir.ActivationFunctionType
+
+P = 128
+PACK = 4
+KP = 512
+N = 512
+GROUPS = S // KP
+HALVES = B // N
+TILES = N // P
+
+
+def tile_equilibrium_mass_balance_s3_kernel(tc, lam, f_words, f_scales, phi, g, m, a_words, a_scales, feed, out):
+    nc = tc.nc
+    with ExitStack() as ctx:
+        sb = ctx.enter_context(tc.tile_pool(name="sb", bufs=1))
+        ps = ctx.enter_context(tc.psum_pool(name="ps", bufs=1))
+        ctx.enter_context(tc.manual_schedule())
+
+        def tiles(name, count, shape, dtype):
+            return [sb.tile(shape, dtype, name="%s%d" % (name, i), align_bytes=64) for i in range(count)]
+
+        banks = [ps.tile([P, N], F32, name="bank%d" % i) for i in range(8)]
+        ident = sb.tile([P, P], F32, name="ident")
+        one = sb.tile([P, 8], F32, name="one")
+        junk = sb.tile([P, 8], F32, name="junk")
+        m_bf = sb.tile([P, GROUPS, PACK], BF16, name="m_bf")
+        m_f32 = sb.tile([P, GROUPS * PACK], F32, name="m_f32")
+        m_frac = sb.tile([P, GROUPS * PACK], F32, name="m_frac")
+        m_pow = sb.tile([P, GROUPS * PACK], F32, name="m_pow")
+        m_log = sb.tile([P, GROUPS * PACK], F32, name="m_log")
+
+        x_raw = [tiles("x_raw%d_" % h, 3, [P, TILES, KP], BF16) for h in range(HALVES)]
+        x_stage = tiles("x_stage", 3, [P, N * PACK], BF16)
+        x_codes = [tiles("x_codes%d_" % h, 3, [P, N], U32) for h in range(HALVES)]
+        x_scales = [tiles("x_scales%d_" % h, 3, [P, N], U8) for h in range(HALVES)]
+        f_raw = tiles("f_raw", GROUPS, [P, 2, 2 * KP], U8)
+        f_perm = tiles("f_perm", GROUPS, [P, 2, 2 * KP], U8)
+        fs_raw = tiles("fs_raw", 2, [P, 2, 2 * KP], U8)
+        fs_perm = tiles("fs_perm", GROUPS, [P, 2, KP], U8)
+        g_raw = tiles("g_raw", GROUPS, [P, PACK, KP], BF16)
+        g_stage = tiles("g_stage", 2, [P, KP * PACK], BF16)
+        g_codes = tiles("g_codes", GROUPS, [P, KP], U32)
+        g_scales = tiles("g_scales", GROUPS, [P, KP], U8)
+        a_sb = sb.tile([P, GROUPS, 2 * E], U8, name="a_sb", align_bytes=64)
+        as_sb = sb.tile([P, GROUPS, E], U8, name="as_sb", align_bytes=64)
+        feed_sb = tiles("feed_sb", HALVES, [P, TILES, E], BF16)
+        n_rows = [tiles("n_rows%d_" % G, HALVES, [P, PACK, N], BF16) for G in range(GROUPS)]
+        n_stage = tiles("n_stage", 3, [P, N * PACK], BF16)
+        n_codes = [tiles("n_codes%d_" % G, HALVES, [P, N], U32) for G in range(GROUPS)]
+        n_scales = [tiles("n_scales%d_" % G, HALVES, [P, N], U8) for G in range(GROUPS)]
+        res = tiles("res", 4, [P, N], F32)
+
+        nc.scalar.dma_start(out=m_bf[:], in_=m.rearrange("(G p t) -> p G t", p=P, t=PACK))
+        nc.vector.memset(one[:], 1.0)
+        nc.vector.memset(fs_raw[0][:].bitcast(I32), 0)
+        nc.scalar.activation(out=junk[:, 0:1], in_=one[:, 0:1], func=ACT.Ln)
+        make_identity(nc, ident[:])
+        nc.vector.memset(fs_raw[1][:].bitcast(I32), 0)
+        nc.vector.memset(as_sb[:].bitcast(I32), 0)
+
+        def load_x(h, c, lo=0, hi=TILES):
+            src = lam[:, c * KP:(c + 1) * KP] if c < 2 else phi
+            rows = src[h * N + lo * P:h * N + hi * P, :]
+            nc.sync.dma_start(out=x_raw[h][c][:, lo:hi, :], in_=rows.rearrange("(b p) k -> p b k", p=P))
+
+        def load_scale_rows(dst, src):
+            for r in range(4):
+                nc.sync.dma_start(out=dst[:].bitcast(I32)[r:P:32, :, :],
+                                  in_=src[:, r:16:4, :].rearrange("c q n -> q c n").bitcast(I32))
+
+        def load_f(G):
+            src = f_words[:, :, G * 2 * KP:(G + 1) * 2 * KP]
+            nc.sync.dma_start(out=f_raw[G][:].bitcast(I32), in_=src.rearrange("c p n -> p c n").bitcast(I32))
+
+        def load_g(G):
+            src = g[:, G * KP:(G + 1) * KP]
+            nc.sync.dma_start(out=g_raw[G][:], in_=src.rearrange("(p j) s -> p j s", j=PACK))
+
+        load_x(0, 0, 0, 2)
+        load_x(0, 0, 2, 4)
+        load_scale_rows(fs_raw[0], f_scales[:, :, 0:2 * KP])
+        load_f(0)
+        load_x(0, 1)
+        load_x(0, 2)
+        load_g(0)
+        for c in range(3):
+            load_x(1, c)
+        load_f(1)
+        load_g(1)
+        load_scale_rows(fs_raw[1], f_scales[:, :, 2 * KP:4 * KP])
+        for G in (2, 3):
+            load_f(G)
+            load_g(G)
+        load_scale_rows(as_sb, a_scales)
+        nc.sync.dma_start(out=a_sb[:].bitcast(I32), in_=a_words.rearrange("c p n -> p c n").bitcast(I32))
+        for h in range(HALVES):
+            nc.sync.dma_start(out=feed_sb[h][:], in_=feed[h * N:(h + 1) * N, :].rearrange("(b p) e -> p b e", p=P))
+
+        nc.vector.tensor_copy(out=m_f32[:], in_=m_bf[:].rearrange("p G t -> p (G t)"))
+        nc.vector.tensor_scalar(out=m_frac[:].bitcast(I32), in0=m_f32[:].bitcast(I32), scalar1=0x007FFFFF, scalar2=0x3F800000,
+                                op0=ALU.bitwise_and, op1=ALU.bitwise_or)
+        nc.vector.tensor_scalar(out=m_pow[:].bitcast(I32), in0=m_f32[:].bitcast(I32), scalar1=23, scalar2=23,
+                                op0=ALU.logical_shift_right, op1=ALU.logical_shift_left)
+        nc.scalar.activation(out=m_log[:], in_=m_frac[:], func=ACT.Ln)
+        nc.scalar.activation(out=junk[:, 1:2], in_=one[:, 0:1], func=ACT.Exp)
+
+        def transpose_x(h, c, first_bank, copy):
+            words = x_raw[h][c][:].bitcast(F32)
+            stage = x_stage[c][:].bitcast(F32)
+            for j in range(2):
+                bank = banks[first_bank + j]
+                for b in range(2):
+                    for u in range(2):
+                        col = (2 * b + u) * P
+                        nc.tensor.transpose(bank[:, col:col + P], words[:, 2 * j + b, u:2 * P:2], ident[:])
+            for j in range(2):
+                copy(out=stage[:, j * N:(j + 1) * N].rearrange("p (b r u) -> p b r u", b=2, u=2),
+                     in_=banks[first_bank + j][:].rearrange("p (b u r) -> p b r u", b=2, u=2))
+
+        def quantize(codes, scales, stage, lo=0, hi=N):
+            nc.vector.quantize_mx(out=codes[:, lo:hi].bitcast(FP8X4), scales=scales[:, lo:hi], in_=stage[:, PACK * lo:PACK * hi])
+
+        def quantize_x(h, c):
+            quantize(x_codes[h][c], x_scales[h][c], x_stage[c])
+
+        def permute_f(G, c):
+            nc.vector.tensor_copy(out=f_perm[G][:, c, :].rearrange("p (t i y) -> p t i y", t=PACK, y=2),
+                                  in_=f_raw[G][:, c, :].rearrange("p (i t y) -> p t i y", t=PACK, y=2))
+            lo = (G % 2) * KP
+            nc.vector.tensor_copy(out=fs_perm[G][:, c, :].rearrange("p (t i) -> p t i", t=PACK),
+                                  in_=fs_raw[G // 2][:, c, lo:lo + KP].rearrange("p (i t) -> p t i", t=PACK))
+
+        def interleave_g(G, copy):
+            copy(out=g_stage[G % 2][:].rearrange("p (t i j) -> p t i j", t=PACK, j=PACK),
+                 in_=g_raw[G][:].rearrange("p j (i t) -> p t i j", t=PACK))
+
+        def quantize_g(G):
+            quantize(g_codes[G], g_scales[G], g_stage[G % 2])
+
+        def z_pass(G, h, t, c, bank):
+            if c < 2:
+                lhsT = f_perm[G][:, c, 2 * P * t:2 * P * (t + 1)].bitcast(FP4X4)
+                lhsT_scale = fs_perm[G][:, c, P * t:P * (t + 1)]
+            else:
+                lhsT = g_codes[G][:, P * t:P * (t + 1)].bitcast(FP8X4)
+                lhsT_scale = g_scales[G][:, P * t:P * (t + 1)]
+            nc.tensor.matmul_mx(out=bank[:], lhsT=lhsT, lhsT_scale=lhsT_scale, rhs=x_codes[h][c][:].bitcast(FP8X4),
+                                rhs_scale=x_scales[h][c][:], start=(c == 0), stop=(c == 2))
+
+        def exp_z(G, h, t, bank):
+            col = PACK * G + t
+            nc.scalar.activation(out=n_rows[G][h][:, t, :], in_=bank[:], func=ACT.Exp, bias=m_log[:, col:col + 1])
+
+        def unit(G, h):
+            for t in range(PACK):
+                bank = banks[PACK * h + t]
+                for c in range(3):
+                    z_pass(G, h, t, c, bank)
+                exp_z(G, h, t, bank)
+
+        def scale_n(G, h):
+            for t in range(PACK):
+                col = PACK * G + t
+                nc.vector.tensor_scalar(out=n_rows[G][h][:, t, :], in0=n_rows[G][h][:, t, :], scalar1=m_pow[:, col:col + 1],
+                                        scalar2=None, op0=ALU.mult)
+
+        def interleave_n(G, h, slot, copy, lo=0, hi=N):
+            copy(out=n_stage[slot][:, PACK * lo:PACK * hi].rearrange("p (b t) -> p b t", t=PACK),
+                 in_=n_rows[G][h][:, :, lo:hi].rearrange("p t b -> p b t"))
+
+        def quantize_n(G, h, slot, lo=0, hi=N):
+            quantize(n_codes[G][h], n_scales[G][h], n_stage[slot], lo, hi)
+
+        def balance(i):
+            bt, eh = divmod(i, 2)
+            h, b = divmod(bt, TILES)
+            bank = banks[i % 8]
+            for G in range(GROUPS):
+                nc.tensor.matmul_mx(out=bank[:], lhsT=n_codes[G][h][:, P * b:P * (b + 1)].bitcast(FP8X4),
+                                    lhsT_scale=n_scales[G][h][:, P * b:P * (b + 1)],
+                                    rhs=a_sb[:, G, 2 * N * eh:2 * N * (eh + 1)].bitcast(FP4X4),
+                                    rhs_scale=as_sb[:, G, N * eh:N * (eh + 1)], start=(G == 0), stop=(G == GROUPS - 1))
+            r = res[i % 4]
+            nc.vector.tensor_tensor(out=r[:], in0=bank[:], in1=feed_sb[h][:, b, N * eh:N * (eh + 1)], op=ALU.subtract)
+            nc.sync.dma_start(out=out[bt * P:(bt + 1) * P, N * eh:N * (eh + 1)], in_=r[:])
+
+        vcopy = nc.vector.tensor_copy
+        scopy = nc.scalar.copy
+
+        transpose_x(0, 0, 4, vcopy)
+        transpose_x(0, 1, 6, scopy)
+        permute_f(0, 0)
+        quantize_x(0, 0)
+        transpose_x(0, 2, 4, scopy)
+        for t in range(PACK):
+            z_pass(0, 0, t, 0, banks[t])
+        permute_f(0, 1)
+        quantize_x(0, 1)
+        transpose_x(1, 0, 6, scopy)
+        for t in range(PACK):
+            z_pass(0, 0, t, 1, banks[t])
+        interleave_g(0, vcopy)
+        quantize_x(0, 2)
+        quantize_g(0)
+        transpose_x(1, 1, 4, scopy)
+        quantize_x(1, 0)
+        transpose_x(1, 2, 6, scopy)
+        for t in range(PACK):
+            z_pass(0, 0, t, 2, banks[t])
+            exp_z(0, 0, t, banks[t])
+        permute_f(1, 0)
+        quantize_x(1, 1)
+        permute_f(1, 1)
+        quantize_x(1, 2)
+        unit(0, 1)
+        interleave_g(1, vcopy)
+        permute_f(2, 0)
+        quantize_g(1)
+        permute_f(2, 1)
+        interleave_g(2, scopy)
+        unit(1, 0)
+        scale_n(0, 0)
+        interleave_n(0, 0, 0, vcopy)
+        scale_n(0, 1)
+        quantize_n(0, 0, 0)
+        interleave_n(0, 1, 1, vcopy)
+        quantize_g(2)
+        quantize_n(0, 1, 1)
+        unit(1, 1)
+        unit(2, 0)
+        permute_f(3, 0)
+        scale_n(1, 0)
+        permute_f(3, 1)
+        interleave_n(1, 0, 2, vcopy)
+        interleave_g(3, vcopy)
+        quantize_n(1, 0, 2)
+        scale_n(1, 1)
+        quantize_g(3)
+        unit(2, 1)
+        unit(3, 0)
+        scale_n(2, 0)
+        interleave_n(1, 1, 0, vcopy)
+        interleave_n(2, 0, 1, vcopy)
+        quantize_n(1, 1, 0)
+        quantize_n(2, 0, 1)
+        scale_n(2, 1)
+        unit(3, 1)
+        scale_n(3, 0)
+        interleave_n(3, 0, 2, vcopy, 0, N // 2)
+        interleave_n(3, 0, 2, vcopy, N // 2, N)
+        quantize_n(3, 0, 2, 0, N // 2)
+        quantize_n(3, 0, 2, N // 2, N)
+        scale_n(3, 1)
+        interleave_n(2, 1, 0, scopy)
+        interleave_n(3, 1, 1, scopy)
+        for i in range(16):
+            balance(i)
+            if i == 2:
+                quantize_n(2, 1, 0)
+            if i == 4:
+                quantize_n(3, 1, 1)

@@ -37,7 +37,9 @@ def tile_equilibrium_mass_balance_s3_kernel(tc, lam, f_words, f_scales, phi, g, 
 
         banks = [ps.tile([P, N], F32, name="bank%d" % i) for i in range(8)]
         ident = sb.tile([P, P], F32, name="ident")
-        one = sb.tile([P, 8], F32, name="one")
+        ones = sb.tile([P, PACK * P], BF16, name="ones", align_bytes=64)
+        warm_codes = sb.tile([P, P], U32, name="warm_codes", align_bytes=64)
+        warm_scales = sb.tile([P, P], U8, name="warm_scales", align_bytes=64)
         junk = sb.tile([P, 8], F32, name="junk")
         m_bf = sb.tile([P, GROUPS, PACK], BF16, name="m_bf")
         m_f32 = sb.tile([P, GROUPS * PACK], F32, name="m_f32")
@@ -51,7 +53,8 @@ def tile_equilibrium_mass_balance_s3_kernel(tc, lam, f_words, f_scales, phi, g, 
         x_scales = [tiles("x_scales%d_" % h, 3, [P, N], U8) for h in range(HALVES)]
         f_raw = tiles("f_raw", GROUPS, [P, 2, 2 * KP], U8)
         f_perm = tiles("f_perm", GROUPS, [P, 2, 2 * KP], U8)
-        fs_raw = tiles("fs_raw", 2, [P, 2, 2 * KP], U8)
+        fs_first = sb.tile([P, 2, KP], U8, name="fs_first", align_bytes=64)
+        fs_rest = sb.tile([P, 2, S - KP], U8, name="fs_rest", align_bytes=64)
         fs_perm = tiles("fs_perm", GROUPS, [P, 2, KP], U8)
         g_raw = tiles("g_raw", GROUPS, [P, PACK, KP], BF16)
         g_stage = tiles("g_stage", 2, [P, KP * PACK], BF16)
@@ -66,27 +69,19 @@ def tile_equilibrium_mass_balance_s3_kernel(tc, lam, f_words, f_scales, phi, g, 
         n_scales = [tiles("n_scales%d_" % G, HALVES, [P, N], U8) for G in range(GROUPS)]
         res = tiles("res", 4, [P, N], F32)
 
-        nc.scalar.dma_start(out=m_bf[:], in_=m.rearrange("(G p t) -> p G t", p=P, t=PACK))
-        nc.vector.memset(one[:], 1.0)
-        nc.vector.memset(fs_raw[0][:].bitcast(I32), 0)
-        nc.scalar.activation(out=junk[:, 0:1], in_=one[:, 0:1], func=ACT.Ln)
-        make_identity(nc, ident[:])
-        nc.vector.memset(fs_raw[1][:].bitcast(I32), 0)
-        nc.vector.memset(as_sb[:].bitcast(I32), 0)
-
         def load_x(h, c, lo=0, hi=TILES):
             src = lam[:, c * KP:(c + 1) * KP] if c < 2 else phi
             rows = src[h * N + lo * P:h * N + hi * P, :]
             nc.sync.dma_start(out=x_raw[h][c][:, lo:hi, :], in_=rows.rearrange("(b p) k -> p b k", p=P))
 
-        def load_scale_rows(dst, src):
+        def load_scale_rows(queue, dst, src):
             for r in range(4):
-                nc.sync.dma_start(out=dst[:].bitcast(I32)[r:P:32, :, :],
-                                  in_=src[:, r:16:4, :].rearrange("c q n -> q c n").bitcast(I32))
+                queue.dma_start(out=dst[:].bitcast(I32)[r:P:32, :, :],
+                                in_=src[:, r:16:4, :].rearrange("c q n -> q c n").bitcast(I32))
 
-        def load_f(G):
-            src = f_words[:, :, G * 2 * KP:(G + 1) * 2 * KP]
-            nc.sync.dma_start(out=f_raw[G][:].bitcast(I32), in_=src.rearrange("c p n -> p c n").bitcast(I32))
+        def load_f(G, lo=0, hi=2):
+            src = f_words[lo:hi, :, G * 2 * KP:(G + 1) * 2 * KP]
+            nc.sync.dma_start(out=f_raw[G][:, lo:hi, :].bitcast(I32), in_=src.rearrange("c p n -> p c n").bitcast(I32))
 
         def load_g(G):
             src = g[:, G * KP:(G + 1) * KP]
@@ -94,20 +89,30 @@ def tile_equilibrium_mass_balance_s3_kernel(tc, lam, f_words, f_scales, phi, g, 
 
         load_x(0, 0, 0, 2)
         load_x(0, 0, 2, 4)
-        load_scale_rows(fs_raw[0], f_scales[:, :, 0:2 * KP])
-        load_f(0)
         load_x(0, 1)
+        nc.scalar.dma_start(out=m_bf[:], in_=m.rearrange("(G p t) -> p G t", p=P, t=PACK))
+        nc.gpsimd.memset(ones[:], 1.0)
+        nc.vector.memset(fs_first[:].bitcast(I32), 0)
+        nc.vector.quantize_mx(out=warm_codes[:].bitcast(FP8X4), scales=warm_scales[:], in_=ones[:])
+        load_scale_rows(nc.scalar, fs_first, f_scales[:, :, 0:KP])
+        nc.scalar.activation(out=junk[:, 0:1], in_=ones[:, 0:1], func=ACT.Ln)
+        make_identity(nc, ident[:])
+        nc.vector.memset(fs_rest[:].bitcast(I32), 0)
+        nc.vector.memset(as_sb[:].bitcast(I32), 0)
+
+        load_f(0)
         load_x(0, 2)
         load_g(0)
-        for c in range(3):
-            load_x(1, c)
+        load_x(1, 0)
+        load_scale_rows(nc.sync, fs_rest, f_scales[:, :, KP:S])
         load_f(1)
+        load_x(1, 1)
+        load_x(1, 2)
         load_g(1)
-        load_scale_rows(fs_raw[1], f_scales[:, :, 2 * KP:4 * KP])
         for G in (2, 3):
             load_f(G)
             load_g(G)
-        load_scale_rows(as_sb, a_scales)
+        load_scale_rows(nc.sync, as_sb, a_scales)
         nc.sync.dma_start(out=a_sb[:].bitcast(I32), in_=a_words.rearrange("c p n -> p c n").bitcast(I32))
         for h in range(HALVES):
             nc.sync.dma_start(out=feed_sb[h][:], in_=feed[h * N:(h + 1) * N, :].rearrange("(b p) e -> p b e", p=P))
@@ -118,20 +123,39 @@ def tile_equilibrium_mass_balance_s3_kernel(tc, lam, f_words, f_scales, phi, g, 
         nc.vector.tensor_scalar(out=m_pow[:].bitcast(I32), in0=m_f32[:].bitcast(I32), scalar1=23, scalar2=23,
                                 op0=ALU.logical_shift_right, op1=ALU.logical_shift_left)
         nc.scalar.activation(out=m_log[:], in_=m_frac[:], func=ACT.Ln)
-        nc.scalar.activation(out=junk[:, 1:2], in_=one[:, 0:1], func=ACT.Exp)
+        nc.scalar.activation(out=junk[:, 1:2], in_=ones[:, 0:1], func=ACT.Exp)
 
-        def transpose_x(h, c, first_bank, copy):
+        def warm(count):
+            for i in range(count):
+                col = (i % PACK) * P
+                nc.tensor.matmul_mx(out=banks[0][:, col:col + P], lhsT=warm_codes[:].bitcast(FP8X4), lhsT_scale=warm_scales[:],
+                                    rhs=warm_codes[:].bitcast(FP8X4), rhs_scale=warm_scales[:], start=True, stop=True)
+
+        def transpose_x(h, c, first_bank):
             words = x_raw[h][c][:].bitcast(F32)
-            stage = x_stage[c][:].bitcast(F32)
             for j in range(2):
                 bank = banks[first_bank + j]
                 for b in range(2):
                     for u in range(2):
                         col = (2 * b + u) * P
                         nc.tensor.transpose(bank[:, col:col + P], words[:, 2 * j + b, u:2 * P:2], ident[:])
+
+        def split_words(c, copy):
+            words = x_raw[1][c][:].bitcast(F32)
+            copy(out=n_stage[c][:].bitcast(F32).rearrange("p (b u i) -> p b u i", b=TILES, u=2),
+                 in_=words.rearrange("p b (i u) -> p b u i", u=2))
+
+        def transpose_split(c, first_bank):
+            words = n_stage[c][:].bitcast(F32)
             for j in range(2):
-                copy(out=stage[:, j * N:(j + 1) * N].rearrange("p (b r u) -> p b r u", b=2, u=2),
-                     in_=banks[first_bank + j][:].rearrange("p (b u r) -> p b r u", b=2, u=2))
+                for q in range(4):
+                    col = (4 * j + q) * P
+                    nc.tensor.transpose(banks[first_bank + j][:, q * P:(q + 1) * P], words[:, col:col + P], ident[:])
+
+        def evacuate_x(c, first_bank, j, copy):
+            stage = x_stage[c][:].bitcast(F32)
+            copy(out=stage[:, j * N:(j + 1) * N].rearrange("p (b r u) -> p b r u", b=2, u=2),
+                 in_=banks[first_bank + j][:].rearrange("p (b u r) -> p b r u", b=2, u=2))
 
         def quantize(codes, scales, stage, lo=0, hi=N):
             nc.vector.quantize_mx(out=codes[:, lo:hi].bitcast(FP8X4), scales=scales[:, lo:hi], in_=stage[:, PACK * lo:PACK * hi])
@@ -139,12 +163,18 @@ def tile_equilibrium_mass_balance_s3_kernel(tc, lam, f_words, f_scales, phi, g, 
         def quantize_x(h, c):
             quantize(x_codes[h][c], x_scales[h][c], x_stage[c])
 
-        def permute_f(G, c):
+        def permute_words(G, c):
             nc.vector.tensor_copy(out=f_perm[G][:, c, :].rearrange("p (t i y) -> p t i y", t=PACK, y=2),
                                   in_=f_raw[G][:, c, :].rearrange("p (i t y) -> p t i y", t=PACK, y=2))
-            lo = (G % 2) * KP
+
+        def permute_scales(G, c):
+            src = fs_first[:, c, :] if G == 0 else fs_rest[:, c, (G - 1) * KP:G * KP]
             nc.vector.tensor_copy(out=fs_perm[G][:, c, :].rearrange("p (t i) -> p t i", t=PACK),
-                                  in_=fs_raw[G // 2][:, c, lo:lo + KP].rearrange("p (i t) -> p t i", t=PACK))
+                                  in_=src.rearrange("p (i t) -> p t i", t=PACK))
+
+        def permute_f(G, c):
+            permute_words(G, c)
+            permute_scales(G, c)
 
         def interleave_g(G, copy):
             copy(out=g_stage[G % 2][:].rearrange("p (t i j) -> p t i j", t=PACK, j=PACK),
@@ -167,9 +197,11 @@ def tile_equilibrium_mass_balance_s3_kernel(tc, lam, f_words, f_scales, phi, g, 
             col = PACK * G + t
             nc.scalar.activation(out=n_rows[G][h][:, t, :], in_=bank[:], func=ACT.Exp, bias=m_log[:, col:col + 1])
 
+        bank_sets = [[2, 3, 6, 7], [0, 4, 5, 1]]
+
         def unit(G, h):
             for t in range(PACK):
-                bank = banks[PACK * h + t]
+                bank = banks[bank_sets[h][t]]
                 for c in range(3):
                     z_pass(G, h, t, c, bank)
                 exp_z(G, h, t, bank)
@@ -181,97 +213,133 @@ def tile_equilibrium_mass_balance_s3_kernel(tc, lam, f_words, f_scales, phi, g, 
                                         scalar2=None, op0=ALU.mult)
 
         def interleave_n(G, h, slot, copy, lo=0, hi=N):
-            copy(out=n_stage[slot][:, PACK * lo:PACK * hi].rearrange("p (b t) -> p b t", t=PACK),
-                 in_=n_rows[G][h][:, :, lo:hi].rearrange("p t b -> p b t"))
+            copy(out=n_stage[slot][:, PACK * lo:PACK * hi].rearrange("p (b i t) -> p b t i", t=PACK, i=4),
+                 in_=n_rows[G][h][:, :, lo:hi].rearrange("p t (b i) -> p b t i", i=4))
 
         def quantize_n(G, h, slot, lo=0, hi=N):
             quantize(n_codes[G][h], n_scales[G][h], n_stage[slot], lo, hi)
 
-        def balance(i):
+        def balance(i, bank, lo, hi, queue):
             bt, eh = divmod(i, 2)
             h, b = divmod(bt, TILES)
-            bank = banks[i % 8]
+            cols = slice(N * eh + lo, N * eh + hi)
             for G in range(GROUPS):
-                nc.tensor.matmul_mx(out=bank[:], lhsT=n_codes[G][h][:, P * b:P * (b + 1)].bitcast(FP8X4),
+                nc.tensor.matmul_mx(out=bank[:, lo:hi], lhsT=n_codes[G][h][:, P * b:P * (b + 1)].bitcast(FP8X4),
                                     lhsT_scale=n_scales[G][h][:, P * b:P * (b + 1)],
-                                    rhs=a_sb[:, G, 2 * N * eh:2 * N * (eh + 1)].bitcast(FP4X4),
-                                    rhs_scale=as_sb[:, G, N * eh:N * (eh + 1)], start=(G == 0), stop=(G == GROUPS - 1))
+                                    rhs=a_sb[:, G, 2 * cols.start:2 * cols.stop].bitcast(FP4X4),
+                                    rhs_scale=as_sb[:, G, cols], start=(G == 0), stop=(G == GROUPS - 1))
             r = res[i % 4]
-            nc.vector.tensor_tensor(out=r[:], in0=bank[:], in1=feed_sb[h][:, b, N * eh:N * (eh + 1)], op=ALU.subtract)
-            nc.sync.dma_start(out=out[bt * P:(bt + 1) * P, N * eh:N * (eh + 1)], in_=r[:])
+            nc.vector.tensor_tensor(out=r[:, lo:hi], in0=bank[:, lo:hi], in1=feed_sb[h][:, b, cols], op=ALU.subtract)
+            queue.dma_start(out=out[bt * P:(bt + 1) * P, cols], in_=r[:, lo:hi])
 
         vcopy = nc.vector.tensor_copy
         scopy = nc.scalar.copy
 
-        transpose_x(0, 0, 4, vcopy)
-        transpose_x(0, 1, 6, scopy)
-        permute_f(0, 0)
+        def z_passes(G, h, c, bank_set):
+            for t in range(PACK):
+                z_pass(G, h, t, c, banks[bank_set[t]])
+
+        first = [0, 1, 2, 3]
+        warm(10)
+        transpose_x(0, 0, 4)
+        permute_scales(0, 0)
+        evacuate_x(0, 4, 0, vcopy)
+        evacuate_x(0, 4, 1, vcopy)
+        permute_scales(0, 1)
         quantize_x(0, 0)
-        transpose_x(0, 2, 4, scopy)
-        for t in range(PACK):
-            z_pass(0, 0, t, 0, banks[t])
-        permute_f(0, 1)
+        permute_words(0, 0)
+        warm(8)
+        transpose_x(0, 1, 6)
+        evacuate_x(1, 6, 0, scopy)
+        evacuate_x(1, 6, 1, scopy)
+        transpose_x(0, 2, 4)
+        evacuate_x(2, 4, 0, scopy)
+        evacuate_x(2, 4, 1, scopy)
+        permute_words(0, 1)
         quantize_x(0, 1)
-        transpose_x(1, 0, 6, scopy)
-        for t in range(PACK):
-            z_pass(0, 0, t, 1, banks[t])
+        z_passes(0, 0, 0, first)
+        z_passes(0, 0, 1, first)
+        split_words(0, scopy)
         interleave_g(0, vcopy)
         quantize_x(0, 2)
         quantize_g(0)
-        transpose_x(1, 1, 4, scopy)
-        quantize_x(1, 0)
-        transpose_x(1, 2, 6, scopy)
-        for t in range(PACK):
-            z_pass(0, 0, t, 2, banks[t])
-            exp_z(0, 0, t, banks[t])
+        split_words(1, scopy)
+        transpose_split(0, 6)
+        evacuate_x(0, 6, 0, scopy)
+        evacuate_x(0, 6, 1, scopy)
+        z_passes(0, 0, 2, first)
         permute_f(1, 0)
+        permute_words(1, 1)
+        split_words(2, vcopy)
+        permute_scales(1, 1)
+        quantize_x(1, 0)
+        transpose_split(1, 4)
+        transpose_split(2, 6)
+        exp_z(0, 0, 0, banks[0])
+        evacuate_x(1, 4, 0, scopy)
+        evacuate_x(1, 4, 1, scopy)
+        for t in range(1, PACK):
+            exp_z(0, 0, t, banks[t])
+        evacuate_x(2, 6, 0, vcopy)
+        evacuate_x(2, 6, 1, vcopy)
         quantize_x(1, 1)
-        permute_f(1, 1)
         quantize_x(1, 2)
-        unit(0, 1)
+        for c in range(3):
+            z_passes(0, 1, c, bank_sets[1])
+        for t in range(PACK):
+            exp_z(0, 1, t, banks[bank_sets[1][t]])
         interleave_g(1, vcopy)
-        permute_f(2, 0)
+        permute_words(2, 0)
         quantize_g(1)
-        permute_f(2, 1)
         interleave_g(2, scopy)
-        unit(1, 0)
+        for c in range(3):
+            z_passes(1, 0, c, bank_sets[0])
+        for t in range(PACK):
+            exp_z(1, 0, t, banks[bank_sets[0][t]])
         scale_n(0, 0)
+        permute_scales(2, 0)
         interleave_n(0, 0, 0, vcopy)
-        scale_n(0, 1)
-        quantize_n(0, 0, 0)
-        interleave_n(0, 1, 1, vcopy)
+        permute_f(2, 1)
         quantize_g(2)
-        quantize_n(0, 1, 1)
+        quantize_n(0, 0, 0)
         unit(1, 1)
         unit(2, 0)
-        permute_f(3, 0)
         scale_n(1, 0)
-        permute_f(3, 1)
+        permute_f(3, 0)
         interleave_n(1, 0, 2, vcopy)
-        interleave_g(3, vcopy)
+        permute_f(3, 1)
         quantize_n(1, 0, 2)
-        scale_n(1, 1)
+        interleave_g(3, vcopy)
+        scale_n(0, 1)
         quantize_g(3)
+        scale_n(2, 0)
         unit(2, 1)
         unit(3, 0)
-        scale_n(2, 0)
-        interleave_n(1, 1, 0, vcopy)
-        interleave_n(2, 0, 1, vcopy)
-        quantize_n(1, 1, 0)
-        quantize_n(2, 0, 1)
+        interleave_n(2, 0, 0, vcopy)
+        scale_n(1, 1)
+        quantize_n(2, 0, 0)
         scale_n(2, 1)
+        interleave_n(0, 1, 1, scopy)
         unit(3, 1)
         scale_n(3, 0)
         interleave_n(3, 0, 2, vcopy, 0, N // 2)
         interleave_n(3, 0, 2, vcopy, N // 2, N)
         quantize_n(3, 0, 2, 0, N // 2)
         quantize_n(3, 0, 2, N // 2, N)
-        scale_n(3, 1)
-        interleave_n(2, 1, 0, scopy)
-        interleave_n(3, 1, 1, scopy)
-        for i in range(16):
-            balance(i)
+        quantize_n(0, 1, 1)
+        interleave_n(1, 1, 0, scopy)
+        interleave_n(2, 1, 1, scopy)
+        order = bank_sets[0] + bank_sets[1]
+        for i in range(15):
+            balance(i, banks[order[i % 8]], 0, N, nc.sync)
+            if i == 0:
+                scale_n(3, 1)
+            if i == 1:
+                interleave_n(3, 1, 2, vcopy)
             if i == 2:
-                quantize_n(2, 1, 0)
+                quantize_n(1, 1, 0)
+                quantize_n(3, 1, 2)
             if i == 4:
-                quantize_n(3, 1, 1)
+                quantize_n(2, 1, 1)
+        for q in range(4):
+            balance(15, banks[order[(7 + q) % 8]], q * P, (q + 1) * P, nc.scalar if q % 2 == 0 else nc.sync)

@@ -37,9 +37,7 @@ def tile_equilibrium_mass_balance_s3_kernel(tc, lam, f_words, f_scales, phi, g, 
 
         banks = [ps.tile([P, N], F32, name="bank%d" % i) for i in range(8)]
         ident = sb.tile([P, P], F32, name="ident")
-        ones = sb.tile([P, PACK * P], BF16, name="ones", align_bytes=64)
-        warm_codes = sb.tile([P, P], U32, name="warm_codes", align_bytes=64)
-        warm_scales = sb.tile([P, P], U8, name="warm_scales", align_bytes=64)
+        ones = sb.tile([P, 8], F32, name="ones")
         junk = sb.tile([P, 8], F32, name="junk")
         m_bf = sb.tile([P, GROUPS, PACK], BF16, name="m_bf")
         m_f32 = sb.tile([P, GROUPS * PACK], F32, name="m_f32")
@@ -47,16 +45,17 @@ def tile_equilibrium_mass_balance_s3_kernel(tc, lam, f_words, f_scales, phi, g, 
         m_pow = sb.tile([P, GROUPS * PACK], F32, name="m_pow")
         m_log = sb.tile([P, GROUPS * PACK], F32, name="m_log")
 
-        x_raw = [tiles("x_raw%d_" % h, 3, [P, TILES, KP], BF16) for h in range(HALVES)]
+        x_raw = [tiles("x_raw%d_" % h, 3, [P, TILES * KP], BF16) for h in range(HALVES)]
         x_stage = tiles("x_stage", 3, [P, N * PACK], BF16)
         x_codes = [tiles("x_codes%d_" % h, 3, [P, N], U32) for h in range(HALVES)]
         x_scales = [tiles("x_scales%d_" % h, 3, [P, N], U8) for h in range(HALVES)]
-        f_raw = tiles("f_raw", GROUPS, [P, 2, 2 * KP], U8)
+        parts = [(0, 1), (1, 2), (2, 4)]
+        f_raw = [sb.tile([P, 2, 2 * KP * (hi - lo)], U8, name="f_raw%d" % lo, align_bytes=64) for lo, hi in parts]
         f_perm = tiles("f_perm", GROUPS, [P, 2, 2 * KP], U8)
         fs_first = sb.tile([P, 2, KP], U8, name="fs_first", align_bytes=64)
         fs_rest = sb.tile([P, 2, S - KP], U8, name="fs_rest", align_bytes=64)
         fs_perm = tiles("fs_perm", GROUPS, [P, 2, KP], U8)
-        g_raw = tiles("g_raw", GROUPS, [P, PACK, KP], BF16)
+        g_raw = [sb.tile([P, PACK, KP * (hi - lo)], BF16, name="g_raw%d" % lo, align_bytes=64) for lo, hi in parts]
         g_stage = tiles("g_stage", 2, [P, KP * PACK], BF16)
         g_codes = tiles("g_codes", GROUPS, [P, KP], U32)
         g_scales = tiles("g_scales", GROUPS, [P, KP], U8)
@@ -69,53 +68,52 @@ def tile_equilibrium_mass_balance_s3_kernel(tc, lam, f_words, f_scales, phi, g, 
         n_scales = [tiles("n_scales%d_" % G, HALVES, [P, N], U8) for G in range(GROUPS)]
         res = tiles("res", 4, [P, N], F32)
 
-        def load_x(h, c, lo=0, hi=TILES):
-            src = lam[:, c * KP:(c + 1) * KP] if c < 2 else phi
-            rows = src[h * N + lo * P:h * N + hi * P, :]
-            nc.sync.dma_start(out=x_raw[h][c][:, lo:hi, :], in_=rows.rearrange("(b p) k -> p b k", p=P))
+        def cells(src, h):
+            return src[h * N:(h + 1) * N, :].rearrange("(p b) k -> p b k", b=TILES)
+
+        def load_x(h, j):
+            src = cells(lam, h)[:, 2 * j:2 * j + 2, :] if j < 2 else cells(phi, h)
+            nc.sync.dma_start(out=x_raw[h][j][:], in_=src.rearrange("p b k -> p (b k)"))
 
         def load_scale_rows(queue, dst, src):
             for r in range(4):
                 queue.dma_start(out=dst[:].bitcast(I32)[r:P:32, :, :],
                                 in_=src[:, r:16:4, :].rearrange("c q n -> q c n").bitcast(I32))
 
-        def load_f(G, lo=0, hi=2):
-            src = f_words[lo:hi, :, G * 2 * KP:(G + 1) * 2 * KP]
-            nc.sync.dma_start(out=f_raw[G][:, lo:hi, :].bitcast(I32), in_=src.rearrange("c p n -> p c n").bitcast(I32))
+        def load_f(part):
+            lo, hi = parts[part]
+            src = f_words[:, :, lo * 2 * KP:hi * 2 * KP]
+            nc.sync.dma_start(out=f_raw[part][:].bitcast(I32), in_=src.rearrange("c p n -> p c n").bitcast(I32))
 
-        def load_g(G):
-            src = g[:, G * KP:(G + 1) * KP]
-            nc.sync.dma_start(out=g_raw[G][:], in_=src.rearrange("(p j) s -> p j s", j=PACK))
+        def load_g(part):
+            lo, hi = parts[part]
+            nc.sync.dma_start(out=g_raw[part][:], in_=g[:, lo * KP:hi * KP].rearrange("(p j) s -> p j s", j=PACK))
 
-        load_x(0, 0, 0, 2)
-        load_x(0, 0, 2, 4)
+        load_x(0, 0)
         load_x(0, 1)
+        load_f(0)
         nc.scalar.dma_start(out=m_bf[:], in_=m.rearrange("(G p t) -> p G t", p=P, t=PACK))
-        nc.gpsimd.memset(ones[:], 1.0)
+        nc.vector.memset(ones[:], 1.0)
         nc.vector.memset(fs_first[:].bitcast(I32), 0)
-        nc.vector.quantize_mx(out=warm_codes[:].bitcast(FP8X4), scales=warm_scales[:], in_=ones[:])
-        load_scale_rows(nc.scalar, fs_first, f_scales[:, :, 0:KP])
+        load_scale_rows(nc.sync, fs_first, f_scales[:, :, 0:KP])
         nc.scalar.activation(out=junk[:, 0:1], in_=ones[:, 0:1], func=ACT.Ln)
         make_identity(nc, ident[:])
         nc.vector.memset(fs_rest[:].bitcast(I32), 0)
         nc.vector.memset(as_sb[:].bitcast(I32), 0)
 
-        load_f(0)
         load_x(0, 2)
         load_g(0)
-        load_x(1, 0)
+        for j in range(3):
+            load_x(1, j)
         load_scale_rows(nc.sync, fs_rest, f_scales[:, :, KP:S])
         load_f(1)
-        load_x(1, 1)
-        load_x(1, 2)
         load_g(1)
-        for G in (2, 3):
-            load_f(G)
-            load_g(G)
+        load_f(2)
+        load_g(2)
         load_scale_rows(nc.sync, as_sb, a_scales)
         nc.sync.dma_start(out=a_sb[:].bitcast(I32), in_=a_words.rearrange("c p n -> p c n").bitcast(I32))
         for h in range(HALVES):
-            nc.sync.dma_start(out=feed_sb[h][:], in_=feed[h * N:(h + 1) * N, :].rearrange("(b p) e -> p b e", p=P))
+            nc.sync.dma_start(out=feed_sb[h][:], in_=cells(feed, h))
 
         nc.vector.tensor_copy(out=m_f32[:], in_=m_bf[:].rearrange("p G t -> p (G t)"))
         nc.vector.tensor_scalar(out=m_frac[:].bitcast(I32), in0=m_f32[:].bitcast(I32), scalar1=0x007FFFFF, scalar2=0x3F800000,
@@ -125,37 +123,34 @@ def tile_equilibrium_mass_balance_s3_kernel(tc, lam, f_words, f_scales, phi, g, 
         nc.scalar.activation(out=m_log[:], in_=m_frac[:], func=ACT.Ln)
         nc.scalar.activation(out=junk[:, 1:2], in_=ones[:, 0:1], func=ACT.Exp)
 
-        def warm(count):
-            for i in range(count):
-                col = (i % PACK) * P
-                nc.tensor.matmul_mx(out=banks[0][:, col:col + P], lhsT=warm_codes[:].bitcast(FP8X4), lhsT_scale=warm_scales[:],
-                                    rhs=warm_codes[:].bitcast(FP8X4), rhs_scale=warm_scales[:], start=True, stop=True)
+        def blocks(j, y):
+            return (y, 2 + y) if j < 2 else (2 * y, 2 * y + 1)
 
-        def transpose_x(h, c, first_bank):
-            words = x_raw[h][c][:].bitcast(F32)
-            for j in range(2):
-                bank = banks[first_bank + j]
-                for b in range(2):
+        def transpose_stepped(j, first_bank):
+            words = x_raw[0][j][:].bitcast(F32).rearrange("p (q w) -> p q w", q=4)
+            for y in range(2):
+                for b, q in enumerate(blocks(j, y)):
                     for u in range(2):
                         col = (2 * b + u) * P
-                        nc.tensor.transpose(bank[:, col:col + P], words[:, 2 * j + b, u:2 * P:2], ident[:])
+                        nc.tensor.transpose(banks[first_bank + y][:, col:col + P], words[:, q, u:2 * P:2], ident[:])
 
-        def split_words(c, copy):
-            words = x_raw[1][c][:].bitcast(F32)
-            copy(out=n_stage[c][:].bitcast(F32).rearrange("p (b u i) -> p b u i", b=TILES, u=2),
-                 in_=words.rearrange("p b (i u) -> p b u i", u=2))
+        def split_words(j, copy):
+            copy(out=n_stage[j][:].bitcast(F32).rearrange("p (q u i) -> p q u i", q=4, u=2),
+                 in_=x_raw[1][j][:].bitcast(F32).rearrange("p (q i u) -> p q u i", q=4, u=2))
 
-        def transpose_split(c, first_bank):
-            words = n_stage[c][:].bitcast(F32)
-            for j in range(2):
-                for q in range(4):
-                    col = (4 * j + q) * P
-                    nc.tensor.transpose(banks[first_bank + j][:, q * P:(q + 1) * P], words[:, col:col + P], ident[:])
+        def transpose_split(j, first_bank):
+            words = n_stage[j][:].bitcast(F32).rearrange("p (q u i) -> p q u i", q=4, u=2)
+            for y in range(2):
+                for b, q in enumerate(blocks(j, y)):
+                    for u in range(2):
+                        col = (2 * b + u) * P
+                        nc.tensor.transpose(banks[first_bank + y][:, col:col + P], words[:, q, u, :], ident[:])
 
-        def evacuate_x(c, first_bank, j, copy):
+        def evacuate_x(j, first_bank, y, copy):
+            c, pair = (y, j) if j < 2 else (2, y)
             stage = x_stage[c][:].bitcast(F32)
-            copy(out=stage[:, j * N:(j + 1) * N].rearrange("p (b r u) -> p b r u", b=2, u=2),
-                 in_=banks[first_bank + j][:].rearrange("p (b u r) -> p b r u", b=2, u=2))
+            copy(out=stage[:, pair * N:(pair + 1) * N].rearrange("p (b r u) -> p b r u", b=2, u=2),
+                 in_=banks[first_bank + y][:].rearrange("p (b u r) -> p b r u", b=2, u=2))
 
         def quantize(codes, scales, stage, lo=0, hi=N):
             nc.vector.quantize_mx(out=codes[:, lo:hi].bitcast(FP8X4), scales=scales[:, lo:hi], in_=stage[:, PACK * lo:PACK * hi])
@@ -164,8 +159,10 @@ def tile_equilibrium_mass_balance_s3_kernel(tc, lam, f_words, f_scales, phi, g, 
             quantize(x_codes[h][c], x_scales[h][c], x_stage[c])
 
         def permute_words(G, c):
+            part = min(G, 2)
+            lo = (G - parts[part][0]) * 2 * KP
             nc.vector.tensor_copy(out=f_perm[G][:, c, :].rearrange("p (t i y) -> p t i y", t=PACK, y=2),
-                                  in_=f_raw[G][:, c, :].rearrange("p (i t y) -> p t i y", t=PACK, y=2))
+                                  in_=f_raw[part][:, c, lo:lo + 2 * KP].rearrange("p (i t y) -> p t i y", t=PACK, y=2))
 
         def permute_scales(G, c):
             src = fs_first[:, c, :] if G == 0 else fs_rest[:, c, (G - 1) * KP:G * KP]
@@ -177,8 +174,10 @@ def tile_equilibrium_mass_balance_s3_kernel(tc, lam, f_words, f_scales, phi, g, 
             permute_scales(G, c)
 
         def interleave_g(G, copy):
-            copy(out=g_stage[G % 2][:].rearrange("p (t i j) -> p t i j", t=PACK, j=PACK),
-                 in_=g_raw[G][:].rearrange("p j (i t) -> p t i j", t=PACK))
+            part = min(G, 2)
+            lo = (G - parts[part][0]) * KP
+            copy(out=g_stage[G % 2][:].rearrange("p (t i j) -> p i t j", t=PACK, j=PACK),
+                 in_=g_raw[part][:, :, lo:lo + KP].rearrange("p j (i t) -> p i t j", t=PACK))
 
         def quantize_g(G):
             quantize(g_codes[G], g_scales[G], g_stage[G % 2])
@@ -197,7 +196,7 @@ def tile_equilibrium_mass_balance_s3_kernel(tc, lam, f_words, f_scales, phi, g, 
             col = PACK * G + t
             nc.scalar.activation(out=n_rows[G][h][:, t, :], in_=bank[:], func=ACT.Exp, bias=m_log[:, col:col + 1])
 
-        bank_sets = [[2, 3, 6, 7], [0, 4, 5, 1]]
+        bank_sets = [[2, 3, 6, 7], [4, 5, 0, 1]]
 
         def unit(G, h):
             for t in range(PACK):
@@ -213,8 +212,8 @@ def tile_equilibrium_mass_balance_s3_kernel(tc, lam, f_words, f_scales, phi, g, 
                                         scalar2=None, op0=ALU.mult)
 
         def interleave_n(G, h, slot, copy, lo=0, hi=N):
-            copy(out=n_stage[slot][:, PACK * lo:PACK * hi].rearrange("p (b i t) -> p b t i", t=PACK, i=4),
-                 in_=n_rows[G][h][:, :, lo:hi].rearrange("p t (b i) -> p b t i", i=4))
+            copy(out=n_stage[slot][:, PACK * lo:PACK * hi].rearrange("p (b t) -> p b t", t=PACK),
+                 in_=n_rows[G][h][:, :, lo:hi].rearrange("p t b -> p b t"))
 
         def quantize_n(G, h, slot, lo=0, hi=N):
             quantize(n_codes[G][h], n_scales[G][h], n_stage[slot], lo, hi)
@@ -230,7 +229,7 @@ def tile_equilibrium_mass_balance_s3_kernel(tc, lam, f_words, f_scales, phi, g, 
                                     rhs_scale=as_sb[:, G, cols], start=(G == 0), stop=(G == GROUPS - 1))
             r = res[i % 4]
             nc.vector.tensor_tensor(out=r[:, lo:hi], in0=bank[:, lo:hi], in1=feed_sb[h][:, b, cols], op=ALU.subtract)
-            queue.dma_start(out=out[bt * P:(bt + 1) * P, cols], in_=r[:, lo:hi])
+            queue.dma_start(out=cells(out, h)[:, b, cols], in_=r[:, lo:hi])
 
         vcopy = nc.vector.tensor_copy
         scopy = nc.scalar.copy
@@ -240,56 +239,52 @@ def tile_equilibrium_mass_balance_s3_kernel(tc, lam, f_words, f_scales, phi, g, 
                 z_pass(G, h, t, c, banks[bank_set[t]])
 
         first = [0, 1, 2, 3]
-        warm(10)
-        transpose_x(0, 0, 4)
-        permute_scales(0, 0)
+        transpose_stepped(0, 4)
+        transpose_stepped(1, 6)
         evacuate_x(0, 4, 0, vcopy)
         evacuate_x(0, 4, 1, vcopy)
-        permute_scales(0, 1)
-        quantize_x(0, 0)
-        permute_words(0, 0)
-        warm(8)
-        transpose_x(0, 1, 6)
-        evacuate_x(1, 6, 0, scopy)
+        evacuate_x(1, 6, 0, vcopy)
         evacuate_x(1, 6, 1, scopy)
-        transpose_x(0, 2, 4)
+        permute_words(0, 0)
+        quantize_x(0, 0)
+        permute_scales(0, 0)
+        transpose_stepped(2, 4)
         evacuate_x(2, 4, 0, scopy)
         evacuate_x(2, 4, 1, scopy)
-        permute_words(0, 1)
+        permute_f(0, 1)
         quantize_x(0, 1)
         z_passes(0, 0, 0, first)
         z_passes(0, 0, 1, first)
         split_words(0, scopy)
+        split_words(1, scopy)
         interleave_g(0, vcopy)
         quantize_x(0, 2)
         quantize_g(0)
-        split_words(1, scopy)
         transpose_split(0, 6)
-        evacuate_x(0, 6, 0, scopy)
-        evacuate_x(0, 6, 1, scopy)
-        z_passes(0, 0, 2, first)
-        permute_f(1, 0)
-        permute_words(1, 1)
-        split_words(2, vcopy)
-        permute_scales(1, 1)
-        quantize_x(1, 0)
         transpose_split(1, 4)
-        transpose_split(2, 6)
-        exp_z(0, 0, 0, banks[0])
+        z_passes(0, 0, 2, first)
+        split_words(2, vcopy)
+        evacuate_x(0, 6, 0, scopy)
         evacuate_x(1, 4, 0, scopy)
+        evacuate_x(0, 6, 1, scopy)
         evacuate_x(1, 4, 1, scopy)
-        for t in range(1, PACK):
+        transpose_split(2, 6)
+        for t in range(PACK):
             exp_z(0, 0, t, banks[t])
+        quantize_x(1, 0)
+        permute_words(1, 0)
+        quantize_x(1, 1)
         evacuate_x(2, 6, 0, vcopy)
         evacuate_x(2, 6, 1, vcopy)
-        quantize_x(1, 1)
+        permute_scales(1, 0)
         quantize_x(1, 2)
         for c in range(3):
             z_passes(0, 1, c, bank_sets[1])
         for t in range(PACK):
             exp_z(0, 1, t, banks[bank_sets[1][t]])
+        permute_f(1, 1)
         interleave_g(1, vcopy)
-        permute_words(2, 0)
+        permute_scales(2, 0)
         quantize_g(1)
         interleave_g(2, scopy)
         for c in range(3):
@@ -297,7 +292,7 @@ def tile_equilibrium_mass_balance_s3_kernel(tc, lam, f_words, f_scales, phi, g, 
         for t in range(PACK):
             exp_z(1, 0, t, banks[bank_sets[0][t]])
         scale_n(0, 0)
-        permute_scales(2, 0)
+        permute_words(2, 0)
         interleave_n(0, 0, 0, vcopy)
         permute_f(2, 1)
         quantize_g(2)

@@ -33,11 +33,13 @@ def tile_equilibrium_mass_balance_s3_kernel(tc, lam, f_words, f_scales, phi, g, 
         ctx.enter_context(tc.manual_schedule())
 
         def tiles(name, count, shape, dtype):
-            return [sb.tile(shape, dtype, name="%s%d" % (name, i), align_bytes=64) for i in range(count)]
+            return [sb.tile(shape, dtype, name="%s%d" % (name, i), align_bytes=256) for i in range(count)]
 
         banks = [ps.tile([P, N], F32, name="bank%d" % i) for i in range(8)]
         ident = sb.tile([P, P], F32, name="ident")
-        ones = sb.tile([P, 8], F32, name="ones")
+        ones = sb.tile([P, PACK * P], BF16, name="ones", align_bytes=256)
+        warm_codes = sb.tile([P, P], U32, name="warm_codes", align_bytes=256)
+        warm_scales = sb.tile([P, P], U8, name="warm_scales", align_bytes=256)
         junk = sb.tile([P, 8], F32, name="junk")
         m_bf = sb.tile([P, GROUPS, PACK], BF16, name="m_bf")
         m_f32 = sb.tile([P, GROUPS * PACK], F32, name="m_f32")
@@ -50,23 +52,23 @@ def tile_equilibrium_mass_balance_s3_kernel(tc, lam, f_words, f_scales, phi, g, 
         x_codes = [tiles("x_codes%d_" % h, 3, [P, N], U32) for h in range(HALVES)]
         x_scales = [tiles("x_scales%d_" % h, 3, [P, N], U8) for h in range(HALVES)]
         parts = [(0, 1), (1, 2), (2, 4)]
-        f_raw = [sb.tile([P, 2, 2 * KP * (hi - lo)], U8, name="f_raw%d" % lo, align_bytes=64) for lo, hi in parts]
+        f_raw = [sb.tile([P, 2, 2 * KP * (hi - lo)], U8, name="f_raw%d" % lo, align_bytes=256) for lo, hi in parts]
         f_perm = tiles("f_perm", GROUPS, [P, 2, 2 * KP], U8)
-        fs_first = sb.tile([P, 2, KP], U8, name="fs_first", align_bytes=64)
-        fs_rest = sb.tile([P, 2, S - KP], U8, name="fs_rest", align_bytes=64)
+        fs_first = sb.tile([P, 2, KP], U8, name="fs_first", align_bytes=256)
+        fs_rest = sb.tile([P, 2, S - KP], U8, name="fs_rest", align_bytes=256)
         fs_perm = tiles("fs_perm", GROUPS, [P, 2, KP], U8)
-        g_raw = [sb.tile([P, PACK, KP * (hi - lo)], BF16, name="g_raw%d" % lo, align_bytes=64) for lo, hi in parts]
+        g_raw = [sb.tile([P, PACK, KP * (hi - lo)], BF16, name="g_raw%d" % lo, align_bytes=256) for lo, hi in parts]
         g_stage = tiles("g_stage", 2, [P, KP * PACK], BF16)
         g_codes = tiles("g_codes", GROUPS, [P, KP], U32)
         g_scales = tiles("g_scales", GROUPS, [P, KP], U8)
-        a_sb = sb.tile([P, GROUPS, 2 * E], U8, name="a_sb", align_bytes=64)
-        as_sb = sb.tile([P, GROUPS, E], U8, name="as_sb", align_bytes=64)
+        a_sb = sb.tile([P, GROUPS, 2 * E], U8, name="a_sb", align_bytes=256)
+        as_sb = sb.tile([P, GROUPS, E], U8, name="as_sb", align_bytes=256)
         feed_sb = tiles("feed_sb", HALVES, [P, TILES, E], BF16)
         n_rows = [tiles("n_rows%d_" % G, HALVES, [P, PACK, N], BF16) for G in range(GROUPS)]
         n_stage = tiles("n_stage", 3, [P, N * PACK], BF16)
         n_codes = [tiles("n_codes%d_" % G, HALVES, [P, N], U32) for G in range(GROUPS)]
         n_scales = [tiles("n_scales%d_" % G, HALVES, [P, N], U8) for G in range(GROUPS)]
-        res = tiles("res", 4, [P, N], F32)
+        res = tiles("res", 8, [P, N], F32)
 
         def cells(src, h):
             return src[h * N:(h + 1) * N, :].rearrange("(p b) k -> p b k", b=TILES)
@@ -98,13 +100,15 @@ def tile_equilibrium_mass_balance_s3_kernel(tc, lam, f_words, f_scales, phi, g, 
         load_scale_rows(nc.sync, fs_first, f_scales[:, :, 0:KP])
         nc.scalar.activation(out=junk[:, 0:1], in_=ones[:, 0:1], func=ACT.Ln)
         make_identity(nc, ident[:])
+        nc.vector.quantize_mx(out=warm_codes[:].bitcast(FP8X4), scales=warm_scales[:], in_=ones[:])
         nc.vector.memset(fs_rest[:].bitcast(I32), 0)
         nc.vector.memset(as_sb[:].bitcast(I32), 0)
 
         load_x(0, 2)
+        load_x(1, 0)
         load_g(0)
-        for j in range(3):
-            load_x(1, j)
+        load_x(1, 1)
+        load_x(1, 2)
         load_scale_rows(nc.sync, fs_rest, f_scales[:, :, KP:S])
         load_f(1)
         load_g(1)
@@ -126,8 +130,8 @@ def tile_equilibrium_mass_balance_s3_kernel(tc, lam, f_words, f_scales, phi, g, 
         def blocks(j, y):
             return (y, 2 + y) if j < 2 else (2 * y, 2 * y + 1)
 
-        def transpose_stepped(j, first_bank):
-            words = x_raw[0][j][:].bitcast(F32).rearrange("p (q w) -> p q w", q=4)
+        def transpose_stepped(h, j, first_bank):
+            words = x_raw[h][j][:].bitcast(F32).rearrange("p (q w) -> p q w", q=4)
             for y in range(2):
                 for b, q in enumerate(blocks(j, y)):
                     for u in range(2):
@@ -227,7 +231,7 @@ def tile_equilibrium_mass_balance_s3_kernel(tc, lam, f_words, f_scales, phi, g, 
                                     lhsT_scale=n_scales[G][h][:, P * b:P * (b + 1)],
                                     rhs=a_sb[:, G, 2 * cols.start:2 * cols.stop].bitcast(FP4X4),
                                     rhs_scale=as_sb[:, G, cols], start=(G == 0), stop=(G == GROUPS - 1))
-            r = res[i % 4]
+            r = res[i % 8]
             nc.vector.tensor_tensor(out=r[:, lo:hi], in0=bank[:, lo:hi], in1=feed_sb[h][:, b, cols], op=ALU.subtract)
             queue.dma_start(out=cells(out, h)[:, b, cols], in_=r[:, lo:hi])
 
@@ -239,16 +243,20 @@ def tile_equilibrium_mass_balance_s3_kernel(tc, lam, f_words, f_scales, phi, g, 
                 z_pass(G, h, t, c, banks[bank_set[t]])
 
         first = [0, 1, 2, 3]
-        transpose_stepped(0, 4)
-        transpose_stepped(1, 6)
+        transpose_stepped(0, 0, 4)
+        transpose_stepped(0, 1, 6)
         evacuate_x(0, 4, 0, vcopy)
-        evacuate_x(0, 4, 1, vcopy)
+        evacuate_x(0, 4, 1, scopy)
         evacuate_x(1, 6, 0, vcopy)
         evacuate_x(1, 6, 1, scopy)
         permute_words(0, 0)
         quantize_x(0, 0)
         permute_scales(0, 0)
-        transpose_stepped(2, 4)
+        for i in range(7):
+            col = (i % PACK) * P
+            nc.tensor.matmul_mx(out=banks[0][:, col:col + P], lhsT=warm_codes[:].bitcast(FP8X4), lhsT_scale=warm_scales[:],
+                                rhs=warm_codes[:].bitcast(FP8X4), rhs_scale=warm_scales[:], start=True, stop=True)
+        transpose_stepped(0, 2, 4)
         evacuate_x(2, 4, 0, scopy)
         evacuate_x(2, 4, 1, scopy)
         permute_f(0, 1)
@@ -256,12 +264,11 @@ def tile_equilibrium_mass_balance_s3_kernel(tc, lam, f_words, f_scales, phi, g, 
         z_passes(0, 0, 0, first)
         z_passes(0, 0, 1, first)
         split_words(0, scopy)
-        split_words(1, scopy)
-        interleave_g(0, vcopy)
         quantize_x(0, 2)
+        interleave_g(0, vcopy)
         quantize_g(0)
         transpose_split(0, 6)
-        transpose_split(1, 4)
+        transpose_stepped(1, 1, 4)
         z_passes(0, 0, 2, first)
         split_words(2, vcopy)
         evacuate_x(0, 6, 0, scopy)
@@ -301,19 +308,18 @@ def tile_equilibrium_mass_balance_s3_kernel(tc, lam, f_words, f_scales, phi, g, 
         unit(2, 0)
         scale_n(1, 0)
         permute_f(3, 0)
-        interleave_n(1, 0, 2, vcopy)
-        permute_f(3, 1)
-        quantize_n(1, 0, 2)
         interleave_g(3, vcopy)
-        scale_n(0, 1)
+        permute_f(3, 1)
         quantize_g(3)
+        interleave_n(1, 0, 2, vcopy)
         scale_n(2, 0)
+        quantize_n(1, 0, 2)
         unit(2, 1)
         unit(3, 0)
         interleave_n(2, 0, 0, vcopy)
-        scale_n(1, 1)
+        scale_n(0, 1)
         quantize_n(2, 0, 0)
-        scale_n(2, 1)
+        scale_n(1, 1)
         interleave_n(0, 1, 1, scopy)
         unit(3, 1)
         scale_n(3, 0)
@@ -321,6 +327,7 @@ def tile_equilibrium_mass_balance_s3_kernel(tc, lam, f_words, f_scales, phi, g, 
         interleave_n(3, 0, 2, vcopy, N // 2, N)
         quantize_n(3, 0, 2, 0, N // 2)
         quantize_n(3, 0, 2, N // 2, N)
+        scale_n(2, 1)
         quantize_n(0, 1, 1)
         interleave_n(1, 1, 0, scopy)
         interleave_n(2, 1, 1, scopy)

@@ -18,11 +18,19 @@ ACT = mybir.ActivationFunctionType
 
 P = 128
 PACK = 4
-KP = 512
+KP = P * PACK
 N = 512
 GROUPS = S // KP
 HALVES = B // N
 TILES = N // P
+PASSES = (E + D) // KP
+PHI = 2
+BANKS = 8
+ALIGN = 256
+PARTS = [(0, 1), (1, 2), (2, 4)]
+FIRST_BANKS = [0, 1, 2, 3]
+Z_BANKS = [[2, 3, 6, 7], [4, 5, 0, 1]]
+WARM_AT_START, WARM_BEFORE_PHI = 14, 8
 
 
 def tile_equilibrium_mass_balance_s3_kernel(tc, lam, f_words, f_scales, phi, g, m, a_words, a_scales, feed, out):
@@ -33,13 +41,13 @@ def tile_equilibrium_mass_balance_s3_kernel(tc, lam, f_words, f_scales, phi, g, 
         ctx.enter_context(tc.manual_schedule())
 
         def tiles(name, count, shape, dtype):
-            return [sb.tile(shape, dtype, name="%s%d" % (name, i), align_bytes=256) for i in range(count)]
+            return [sb.tile(shape, dtype, name="%s%d" % (name, i), align_bytes=ALIGN) for i in range(count)]
 
-        banks = [ps.tile([P, N], F32, name="bank%d" % i) for i in range(8)]
+        banks = [ps.tile([P, N], F32, name="bank%d" % i) for i in range(BANKS)]
         ident = sb.tile([P, P], F32, name="ident")
-        ones = sb.tile([P, PACK * P], BF16, name="ones", align_bytes=256)
-        warm_codes = sb.tile([P, P], U32, name="warm_codes", align_bytes=256)
-        warm_scales = sb.tile([P, P], U8, name="warm_scales", align_bytes=256)
+        ones = sb.tile([P, PACK * P], BF16, name="ones", align_bytes=ALIGN)
+        warm_codes = sb.tile([P, P], U32, name="warm_codes", align_bytes=ALIGN)
+        warm_scales = sb.tile([P, P], U8, name="warm_scales", align_bytes=ALIGN)
         junk = sb.tile([P, 8], F32, name="junk")
         m_bf = sb.tile([P, GROUPS, PACK], BF16, name="m_bf")
         m_f32 = sb.tile([P, GROUPS * PACK], F32, name="m_f32")
@@ -48,112 +56,117 @@ def tile_equilibrium_mass_balance_s3_kernel(tc, lam, f_words, f_scales, phi, g, 
         m_log = sb.tile([P, GROUPS * PACK], F32, name="m_log")
 
         x_raw = [tiles("x_raw%d_" % h, 3, [P, TILES * KP], BF16) for h in range(HALVES)]
-        x_stage = tiles("x_stage", 3, [P, N * PACK], BF16)
-        x_codes = [tiles("x_codes%d_" % h, 3, [P, N], U32) for h in range(HALVES)]
-        x_scales = [tiles("x_scales%d_" % h, 3, [P, N], U8) for h in range(HALVES)]
-        parts = [(0, 1), (1, 2), (2, 4)]
-        f_raw = [sb.tile([P, 2, 2 * KP * (hi - lo)], U8, name="f_raw%d" % lo, align_bytes=256) for lo, hi in parts]
+        x_stage = tiles("x_stage", PASSES, [P, N * PACK], BF16)
+        x_codes = [tiles("x_codes%d_" % h, PASSES, [P, N], U32) for h in range(HALVES)]
+        x_scales = [tiles("x_scales%d_" % h, PASSES, [P, N], U8) for h in range(HALVES)]
+        f_raw = [sb.tile([P, 2, 2 * KP * (hi - lo)], U8, name="f_raw%d" % lo, align_bytes=ALIGN) for lo, hi in PARTS]
         f_perm = tiles("f_perm", GROUPS, [P, 2, 2 * KP], U8)
-        fs_first = sb.tile([P, 2, KP], U8, name="fs_first", align_bytes=256)
-        fs_rest = sb.tile([P, 2, S - KP], U8, name="fs_rest", align_bytes=256)
+        fs_first = sb.tile([P, 2, KP], U8, name="fs_first", align_bytes=ALIGN)
+        fs_rest = sb.tile([P, 2, S - KP], U8, name="fs_rest", align_bytes=ALIGN)
         fs_perm = tiles("fs_perm", GROUPS, [P, 2, KP], U8)
-        g_raw = [sb.tile([P, PACK, KP * (hi - lo)], BF16, name="g_raw%d" % lo, align_bytes=256) for lo, hi in parts]
+        g_raw = [sb.tile([P, PACK, KP * (hi - lo)], BF16, name="g_raw%d" % lo, align_bytes=ALIGN) for lo, hi in PARTS]
         g_stage = tiles("g_stage", 2, [P, KP * PACK], BF16)
         g_codes = tiles("g_codes", GROUPS, [P, KP], U32)
         g_scales = tiles("g_scales", GROUPS, [P, KP], U8)
-        a_sb = sb.tile([P, GROUPS, 2 * E], U8, name="a_sb", align_bytes=256)
-        as_sb = sb.tile([P, GROUPS, E], U8, name="as_sb", align_bytes=256)
+        a_sb = sb.tile([P, GROUPS, 2 * E], U8, name="a_sb", align_bytes=ALIGN)
+        as_sb = sb.tile([P, GROUPS, E], U8, name="as_sb", align_bytes=ALIGN)
         feed_sb = tiles("feed_sb", HALVES, [P, TILES, E], BF16)
         n_rows = [tiles("n_rows%d_" % G, HALVES, [P, PACK, N], BF16) for G in range(GROUPS)]
         n_stage = tiles("n_stage", 3, [P, N * PACK], BF16)
         n_codes = [tiles("n_codes%d_" % G, HALVES, [P, N], U32) for G in range(GROUPS)]
         n_scales = [tiles("n_scales%d_" % G, HALVES, [P, N], U8) for G in range(GROUPS)]
-        res = tiles("res", 8, [P, N], F32)
+        res = tiles("res", BANKS, [P, N], F32)
+
+        vector_copy = nc.vector.tensor_copy
+        scalar_copy = nc.scalar.copy
 
         def cells(src, h):
             return src[h * N:(h + 1) * N, :].rearrange("(p b) k -> p b k", b=TILES)
 
         def load_x(h, j):
-            src = cells(lam, h)[:, 2 * j:2 * j + 2, :] if j < 2 else cells(phi, h)
+            src = cells(phi, h) if j == PHI else cells(lam, h)[:, 2 * j:2 * j + 2, :]
             nc.sync.dma_start(out=x_raw[h][j][:], in_=src.rearrange("p b k -> p (b k)"))
 
-        def load_scale_rows(queue, dst, src):
+        def load_scale_rows(dst, src):
             for r in range(4):
-                queue.dma_start(out=dst[:].bitcast(I32)[r:P:32, :, :],
-                                in_=src[:, r:16:4, :].rearrange("c q n -> q c n").bitcast(I32))
+                nc.sync.dma_start(out=dst[:].bitcast(I32)[r:P:32, :, :],
+                                  in_=src[:, r:16:4, :].rearrange("c q n -> q c n").bitcast(I32))
 
         def load_f(part):
-            lo, hi = parts[part]
+            lo, hi = PARTS[part]
             src = f_words[:, :, lo * 2 * KP:hi * 2 * KP]
             nc.sync.dma_start(out=f_raw[part][:].bitcast(I32), in_=src.rearrange("c p n -> p c n").bitcast(I32))
 
         def load_g(part):
-            lo, hi = parts[part]
+            lo, hi = PARTS[part]
             nc.sync.dma_start(out=g_raw[part][:], in_=g[:, lo * KP:hi * KP].rearrange("(p j) s -> p j s", j=PACK))
 
         load_x(0, 0)
         load_x(0, 1)
         load_f(0)
         nc.scalar.dma_start(out=m_bf[:], in_=m.rearrange("(G p t) -> p G t", p=P, t=PACK))
-        nc.vector.memset(ones[:], 1.0)
+        nc.gpsimd.memset(ones[:], 1.0)
         nc.vector.memset(fs_first[:].bitcast(I32), 0)
-        load_scale_rows(nc.sync, fs_first, f_scales[:, :, 0:KP])
+        nc.vector.quantize_mx(out=warm_codes[:].bitcast(FP8X4), scales=warm_scales[:], in_=ones[:])
+        load_scale_rows(fs_first, f_scales[:, :, 0:KP])
         nc.scalar.activation(out=junk[:, 0:1], in_=ones[:, 0:1], func=ACT.Ln)
         make_identity(nc, ident[:])
-        nc.vector.quantize_mx(out=warm_codes[:].bitcast(FP8X4), scales=warm_scales[:], in_=ones[:])
         nc.vector.memset(fs_rest[:].bitcast(I32), 0)
         nc.vector.memset(as_sb[:].bitcast(I32), 0)
 
-        load_x(0, 2)
+        load_x(0, PHI)
         load_x(1, 0)
         load_g(0)
         load_x(1, 1)
-        load_x(1, 2)
-        load_scale_rows(nc.sync, fs_rest, f_scales[:, :, KP:S])
-        load_f(1)
-        load_g(1)
-        load_f(2)
-        load_g(2)
-        load_scale_rows(nc.sync, as_sb, a_scales)
+        load_x(1, PHI)
+        load_scale_rows(fs_rest, f_scales[:, :, KP:S])
+        for part in (1, 2):
+            load_f(part)
+            load_g(part)
+        load_scale_rows(as_sb, a_scales)
         nc.sync.dma_start(out=a_sb[:].bitcast(I32), in_=a_words.rearrange("c p n -> p c n").bitcast(I32))
         for h in range(HALVES):
             nc.sync.dma_start(out=feed_sb[h][:], in_=cells(feed, h))
 
+        mantissa_bits, bits_of_one, mantissa_width = 0x007FFFFF, 0x3F800000, 23
         nc.vector.tensor_copy(out=m_f32[:], in_=m_bf[:].rearrange("p G t -> p (G t)"))
-        nc.vector.tensor_scalar(out=m_frac[:].bitcast(I32), in0=m_f32[:].bitcast(I32), scalar1=0x007FFFFF, scalar2=0x3F800000,
-                                op0=ALU.bitwise_and, op1=ALU.bitwise_or)
-        nc.vector.tensor_scalar(out=m_pow[:].bitcast(I32), in0=m_f32[:].bitcast(I32), scalar1=23, scalar2=23,
-                                op0=ALU.logical_shift_right, op1=ALU.logical_shift_left)
+        nc.vector.tensor_scalar(out=m_frac[:].bitcast(I32), in0=m_f32[:].bitcast(I32), scalar1=mantissa_bits,
+                                scalar2=bits_of_one, op0=ALU.bitwise_and, op1=ALU.bitwise_or)
+        nc.vector.tensor_scalar(out=m_pow[:].bitcast(I32), in0=m_f32[:].bitcast(I32), scalar1=mantissa_width,
+                                scalar2=mantissa_width, op0=ALU.logical_shift_right, op1=ALU.logical_shift_left)
         nc.scalar.activation(out=m_log[:], in_=m_frac[:], func=ACT.Ln)
         nc.scalar.activation(out=junk[:, 1:2], in_=ones[:, 0:1], func=ACT.Exp)
 
-        def blocks(j, y):
-            return (y, 2 + y) if j < 2 else (2 * y, 2 * y + 1)
+        def warm(count):
+            for i in range(count):
+                col = (i % PACK) * P
+                nc.tensor.matmul_mx(out=banks[0][:, col:col + P], lhsT=warm_codes[:].bitcast(FP8X4), lhsT_scale=warm_scales[:],
+                                    rhs=warm_codes[:].bitcast(FP8X4), rhs_scale=warm_scales[:], start=True, stop=True)
 
-        def transpose_stepped(h, j, first_bank):
-            words = x_raw[h][j][:].bitcast(F32).rearrange("p (q w) -> p q w", q=4)
+        def transpose_pairs(pairs_of, j, first_bank):
             for y in range(2):
-                for b, q in enumerate(blocks(j, y)):
+                runs = (2 * y, 2 * y + 1) if j == PHI else (y, 2 + y)
+                for b, q in enumerate(runs):
                     for u in range(2):
                         col = (2 * b + u) * P
-                        nc.tensor.transpose(banks[first_bank + y][:, col:col + P], words[:, q, u:2 * P:2], ident[:])
+                        nc.tensor.transpose(banks[first_bank + y][:, col:col + P], pairs_of(q, u), ident[:])
 
-        def split_words(j, copy):
+        def transpose_stepped(h, j, first_bank):
+            pairs = x_raw[h][j][:].bitcast(F32).rearrange("p (q w) -> p q w", q=4)
+            transpose_pairs(lambda q, u: pairs[:, q, u:2 * P:2], j, first_bank)
+
+        def split_pairs(j, copy):
             copy(out=n_stage[j][:].bitcast(F32).rearrange("p (q u i) -> p q u i", q=4, u=2),
                  in_=x_raw[1][j][:].bitcast(F32).rearrange("p (q i u) -> p q u i", q=4, u=2))
 
         def transpose_split(j, first_bank):
-            words = n_stage[j][:].bitcast(F32).rearrange("p (q u i) -> p q u i", q=4, u=2)
-            for y in range(2):
-                for b, q in enumerate(blocks(j, y)):
-                    for u in range(2):
-                        col = (2 * b + u) * P
-                        nc.tensor.transpose(banks[first_bank + y][:, col:col + P], words[:, q, u, :], ident[:])
+            pairs = n_stage[j][:].bitcast(F32).rearrange("p (q u i) -> p q u i", q=4, u=2)
+            transpose_pairs(lambda q, u: pairs[:, q, u, :], j, first_bank)
 
         def evacuate_x(j, first_bank, y, copy):
-            c, pair = (y, j) if j < 2 else (2, y)
+            c, tile_pair = (PHI, y) if j == PHI else (y, j)
             stage = x_stage[c][:].bitcast(F32)
-            copy(out=stage[:, pair * N:(pair + 1) * N].rearrange("p (b r u) -> p b r u", b=2, u=2),
+            copy(out=stage[:, tile_pair * N:(tile_pair + 1) * N].rearrange("p (b r u) -> p b r u", b=2, u=2),
                  in_=banks[first_bank + y][:].rearrange("p (b u r) -> p b r u", b=2, u=2))
 
         def quantize(codes, scales, stage, lo=0, hi=N):
@@ -162,11 +175,15 @@ def tile_equilibrium_mass_balance_s3_kernel(tc, lam, f_words, f_scales, phi, g, 
         def quantize_x(h, c):
             quantize(x_codes[h][c], x_scales[h][c], x_stage[c])
 
+        def part_of(G):
+            part = min(G, len(PARTS) - 1)
+            return part, G - PARTS[part][0]
+
         def permute_words(G, c):
-            part = min(G, 2)
-            lo = (G - parts[part][0]) * 2 * KP
+            part, at = part_of(G)
+            src = f_raw[part][:, c, at * 2 * KP:(at + 1) * 2 * KP]
             nc.vector.tensor_copy(out=f_perm[G][:, c, :].rearrange("p (t i y) -> p t i y", t=PACK, y=2),
-                                  in_=f_raw[part][:, c, lo:lo + 2 * KP].rearrange("p (i t y) -> p t i y", t=PACK, y=2))
+                                  in_=src.rearrange("p (i t y) -> p t i y", t=PACK, y=2))
 
         def permute_scales(G, c):
             src = fs_first[:, c, :] if G == 0 else fs_rest[:, c, (G - 1) * KP:G * KP]
@@ -178,36 +195,45 @@ def tile_equilibrium_mass_balance_s3_kernel(tc, lam, f_words, f_scales, phi, g, 
             permute_scales(G, c)
 
         def interleave_g(G, copy):
-            part = min(G, 2)
-            lo = (G - parts[part][0]) * KP
+            part, at = part_of(G)
             copy(out=g_stage[G % 2][:].rearrange("p (t i j) -> p i t j", t=PACK, j=PACK),
-                 in_=g_raw[part][:, :, lo:lo + KP].rearrange("p j (i t) -> p i t j", t=PACK))
+                 in_=g_raw[part][:, :, at * KP:(at + 1) * KP].rearrange("p j (i t) -> p i t j", t=PACK))
 
         def quantize_g(G):
             quantize(g_codes[G], g_scales[G], g_stage[G % 2])
 
         def z_pass(G, h, t, c, bank):
-            if c < 2:
-                lhsT = f_perm[G][:, c, 2 * P * t:2 * P * (t + 1)].bitcast(FP4X4)
-                lhsT_scale = fs_perm[G][:, c, P * t:P * (t + 1)]
-            else:
+            if c == PHI:
                 lhsT = g_codes[G][:, P * t:P * (t + 1)].bitcast(FP8X4)
                 lhsT_scale = g_scales[G][:, P * t:P * (t + 1)]
-            nc.tensor.matmul_mx(out=bank[:], lhsT=lhsT, lhsT_scale=lhsT_scale, rhs=x_codes[h][c][:].bitcast(FP8X4),
-                                rhs_scale=x_scales[h][c][:], start=(c == 0), stop=(c == 2))
+            else:
+                lhsT = f_perm[G][:, c, 2 * P * t:2 * P * (t + 1)].bitcast(FP4X4)
+                lhsT_scale = fs_perm[G][:, c, P * t:P * (t + 1)]
+            nc.tensor.matmul_mx(out=banks[bank][:], lhsT=lhsT, lhsT_scale=lhsT_scale, rhs=x_codes[h][c][:].bitcast(FP8X4),
+                                rhs_scale=x_scales[h][c][:], start=(c == 0), stop=(c == PASSES - 1))
 
         def exp_z(G, h, t, bank):
             col = PACK * G + t
-            nc.scalar.activation(out=n_rows[G][h][:, t, :], in_=bank[:], func=ACT.Exp, bias=m_log[:, col:col + 1])
+            nc.scalar.activation(out=n_rows[G][h][:, t, :], in_=banks[bank][:], func=ACT.Exp, bias=m_log[:, col:col + 1])
 
-        bank_sets = [[2, 3, 6, 7], [4, 5, 0, 1]]
-
-        def unit(G, h):
+        def pass_of_all_t(G, h, c, bank_set):
             for t in range(PACK):
-                bank = banks[bank_sets[h][t]]
-                for c in range(3):
-                    z_pass(G, h, t, c, bank)
-                exp_z(G, h, t, bank)
+                z_pass(G, h, t, c, bank_set[t])
+
+        def exp_of_all_t(G, h, bank_set):
+            for t in range(PACK):
+                exp_z(G, h, t, bank_set[t])
+
+        def z_by_pass(G, h):
+            for c in range(PASSES):
+                pass_of_all_t(G, h, c, Z_BANKS[h])
+            exp_of_all_t(G, h, Z_BANKS[h])
+
+        def z_by_bank(G, h):
+            for t in range(PACK):
+                for c in range(PASSES):
+                    z_pass(G, h, t, c, Z_BANKS[h][t])
+                exp_z(G, h, t, Z_BANKS[h][t])
 
         def scale_n(G, h):
             for t in range(PACK):
@@ -223,125 +249,112 @@ def tile_equilibrium_mass_balance_s3_kernel(tc, lam, f_words, f_scales, phi, g, 
             quantize(n_codes[G][h], n_scales[G][h], n_stage[slot], lo, hi)
 
         def balance(i, bank, lo, hi, queue):
-            bt, eh = divmod(i, 2)
-            h, b = divmod(bt, TILES)
-            cols = slice(N * eh + lo, N * eh + hi)
+            cell_tile, e_half = divmod(i, 2)
+            h, b = divmod(cell_tile, TILES)
+            cols = slice(N * e_half + lo, N * e_half + hi)
             for G in range(GROUPS):
-                nc.tensor.matmul_mx(out=bank[:, lo:hi], lhsT=n_codes[G][h][:, P * b:P * (b + 1)].bitcast(FP8X4),
+                nc.tensor.matmul_mx(out=banks[bank][:, lo:hi], lhsT=n_codes[G][h][:, P * b:P * (b + 1)].bitcast(FP8X4),
                                     lhsT_scale=n_scales[G][h][:, P * b:P * (b + 1)],
                                     rhs=a_sb[:, G, 2 * cols.start:2 * cols.stop].bitcast(FP4X4),
                                     rhs_scale=as_sb[:, G, cols], start=(G == 0), stop=(G == GROUPS - 1))
-            r = res[i % 8]
-            nc.vector.tensor_tensor(out=r[:, lo:hi], in0=bank[:, lo:hi], in1=feed_sb[h][:, b, cols], op=ALU.subtract)
-            queue.dma_start(out=cells(out, h)[:, b, cols], in_=r[:, lo:hi])
+            result = res[i % BANKS]
+            nc.vector.tensor_tensor(out=result[:, lo:hi], in0=banks[bank][:, lo:hi], in1=feed_sb[h][:, b, cols], op=ALU.subtract)
+            queue.dma_start(out=cells(out, h)[:, b, cols], in_=result[:, lo:hi])
 
-        vcopy = nc.vector.tensor_copy
-        scopy = nc.scalar.copy
 
-        def z_passes(G, h, c, bank_set):
-            for t in range(PACK):
-                z_pass(G, h, t, c, banks[bank_set[t]])
-
-        first = [0, 1, 2, 3]
+        warm(WARM_AT_START)
         transpose_stepped(0, 0, 4)
         transpose_stepped(0, 1, 6)
-        evacuate_x(0, 4, 0, vcopy)
-        evacuate_x(0, 4, 1, scopy)
-        evacuate_x(1, 6, 0, vcopy)
-        evacuate_x(1, 6, 1, scopy)
+        evacuate_x(0, 4, 0, vector_copy)
+        evacuate_x(0, 4, 1, scalar_copy)
+        evacuate_x(1, 6, 0, vector_copy)
+        evacuate_x(1, 6, 1, scalar_copy)
         permute_words(0, 0)
         quantize_x(0, 0)
         permute_scales(0, 0)
-        for i in range(7):
-            col = (i % PACK) * P
-            nc.tensor.matmul_mx(out=banks[0][:, col:col + P], lhsT=warm_codes[:].bitcast(FP8X4), lhsT_scale=warm_scales[:],
-                                rhs=warm_codes[:].bitcast(FP8X4), rhs_scale=warm_scales[:], start=True, stop=True)
-        transpose_stepped(0, 2, 4)
-        evacuate_x(2, 4, 0, scopy)
-        evacuate_x(2, 4, 1, scopy)
+        warm(WARM_BEFORE_PHI)
+        transpose_stepped(0, PHI, 4)
+        evacuate_x(PHI, 4, 0, scalar_copy)
+        evacuate_x(PHI, 4, 1, scalar_copy)
         permute_f(0, 1)
         quantize_x(0, 1)
-        z_passes(0, 0, 0, first)
-        z_passes(0, 0, 1, first)
-        split_words(0, scopy)
-        quantize_x(0, 2)
-        interleave_g(0, vcopy)
+        pass_of_all_t(0, 0, 0, FIRST_BANKS)
+        pass_of_all_t(0, 0, 1, FIRST_BANKS)
+
+        split_pairs(0, scalar_copy)
+        quantize_x(0, PHI)
+        interleave_g(0, vector_copy)
         quantize_g(0)
         transpose_split(0, 6)
         transpose_stepped(1, 1, 4)
-        z_passes(0, 0, 2, first)
-        split_words(2, vcopy)
-        evacuate_x(0, 6, 0, scopy)
-        evacuate_x(1, 4, 0, scopy)
-        evacuate_x(0, 6, 1, scopy)
-        evacuate_x(1, 4, 1, scopy)
-        transpose_split(2, 6)
-        for t in range(PACK):
-            exp_z(0, 0, t, banks[t])
+        pass_of_all_t(0, 0, PHI, FIRST_BANKS)
+        split_pairs(PHI, vector_copy)
+        for y in range(2):
+            evacuate_x(0, 6, y, scalar_copy)
+            evacuate_x(1, 4, y, scalar_copy)
+        transpose_split(PHI, 6)
+        exp_of_all_t(0, 0, FIRST_BANKS)
         quantize_x(1, 0)
         permute_words(1, 0)
         quantize_x(1, 1)
-        evacuate_x(2, 6, 0, vcopy)
-        evacuate_x(2, 6, 1, vcopy)
+        evacuate_x(PHI, 6, 0, vector_copy)
+        evacuate_x(PHI, 6, 1, vector_copy)
         permute_scales(1, 0)
-        quantize_x(1, 2)
-        for c in range(3):
-            z_passes(0, 1, c, bank_sets[1])
-        for t in range(PACK):
-            exp_z(0, 1, t, banks[bank_sets[1][t]])
+        quantize_x(1, PHI)
+        z_by_pass(0, 1)
+
         permute_f(1, 1)
-        interleave_g(1, vcopy)
+        interleave_g(1, vector_copy)
         permute_scales(2, 0)
         quantize_g(1)
-        interleave_g(2, scopy)
-        for c in range(3):
-            z_passes(1, 0, c, bank_sets[0])
-        for t in range(PACK):
-            exp_z(1, 0, t, banks[bank_sets[0][t]])
+        interleave_g(2, scalar_copy)
+        z_by_pass(1, 0)
         scale_n(0, 0)
         permute_words(2, 0)
-        interleave_n(0, 0, 0, vcopy)
+        interleave_n(0, 0, 0, vector_copy)
         permute_f(2, 1)
         quantize_g(2)
         quantize_n(0, 0, 0)
-        unit(1, 1)
-        unit(2, 0)
+        z_by_bank(1, 1)
+        z_by_bank(2, 0)
         scale_n(1, 0)
         permute_f(3, 0)
-        interleave_g(3, vcopy)
+        interleave_g(3, vector_copy)
         permute_f(3, 1)
         quantize_g(3)
-        interleave_n(1, 0, 2, vcopy)
+        interleave_n(1, 0, 2, vector_copy)
         scale_n(2, 0)
         quantize_n(1, 0, 2)
-        unit(2, 1)
-        unit(3, 0)
-        interleave_n(2, 0, 0, vcopy)
+        z_by_bank(2, 1)
+        z_by_bank(3, 0)
+        interleave_n(2, 0, 0, vector_copy)
         scale_n(0, 1)
         quantize_n(2, 0, 0)
         scale_n(1, 1)
-        interleave_n(0, 1, 1, scopy)
-        unit(3, 1)
+        interleave_n(0, 1, 1, scalar_copy)
+        z_by_bank(3, 1)
         scale_n(3, 0)
-        interleave_n(3, 0, 2, vcopy, 0, N // 2)
-        interleave_n(3, 0, 2, vcopy, N // 2, N)
-        quantize_n(3, 0, 2, 0, N // 2)
-        quantize_n(3, 0, 2, N // 2, N)
+        pieces = [(0, N // 2), (N // 2, N)]
+        for lo, hi in pieces:
+            interleave_n(3, 0, 2, vector_copy, lo, hi)
+        for lo, hi in pieces:
+            quantize_n(3, 0, 2, lo, hi)
         scale_n(2, 1)
         quantize_n(0, 1, 1)
-        interleave_n(1, 1, 0, scopy)
-        interleave_n(2, 1, 1, scopy)
-        order = bank_sets[0] + bank_sets[1]
-        for i in range(15):
-            balance(i, banks[order[i % 8]], 0, N, nc.sync)
-            if i == 0:
-                scale_n(3, 1)
-            if i == 1:
-                interleave_n(3, 1, 2, vcopy)
-            if i == 2:
-                quantize_n(1, 1, 0)
-                quantize_n(3, 1, 2)
-            if i == 4:
-                quantize_n(2, 1, 1)
-        for q in range(4):
-            balance(15, banks[order[(7 + q) % 8]], q * P, (q + 1) * P, nc.scalar if q % 2 == 0 else nc.sync)
+        interleave_n(1, 1, 0, scalar_copy)
+        interleave_n(2, 1, 1, scalar_copy)
+
+        ring = Z_BANKS[0] + Z_BANKS[1]
+        after_block = {
+            0: [lambda: scale_n(3, 1)],
+            1: [lambda: interleave_n(3, 1, 2, vector_copy)],
+            2: [lambda: quantize_n(1, 1, 0), lambda: quantize_n(3, 1, 2)],
+            4: [lambda: quantize_n(2, 1, 1)],
+        }
+        last = 2 * HALVES * TILES - 1
+        for i in range(last):
+            balance(i, ring[i % BANKS], 0, N, nc.sync)
+            for step in after_block.get(i, []):
+                step()
+        for q in range(N // P):
+            balance(last, ring[(last + q) % BANKS], q * P, (q + 1) * P, nc.scalar if q % 2 == 0 else nc.sync)

from contextlib import ExitStack

import concourse.mybir as mybir
from concourse.masks import make_identity

B, E, D, S = 1024, 1024, 512, 2048
FLOPS = 2 * B * S * (E + D) + 2 * B * E * S

F32 = mybir.dt.float32
BF16 = mybir.dt.bfloat16
I32 = mybir.dt.int32
U32 = mybir.dt.uint32
U8 = mybir.dt.uint8
FP8X4 = mybir.dt.float8_e4m3fn_x4
FP4X4 = mybir.dt.float4_e2m1fn_x4
ALU = mybir.AluOpType
ACT = mybir.ActivationFunctionType

P = 128
PACK = 4
KP = P * PACK
N = 512
GROUPS = S // KP
HALVES = B // N
TILES = N // P
PASSES = (E + D) // KP
PHI = 2
BANKS = 8
ALIGN = 256
PARTS = [(0, 1), (1, 2), (2, 4)]
FIRST_BANKS = [0, 1, 2, 3]
Z_BANKS = [[2, 3, 6, 7], [4, 5, 0, 1]]
WARM_AT_START, WARM_BEFORE_PHI = 14, 8


def tile_equilibrium_mass_balance_s3_kernel(tc, lam, f_words, f_scales, phi, g, m, a_words, a_scales, feed, out):
    nc = tc.nc
    with ExitStack() as ctx:
        sb = ctx.enter_context(tc.tile_pool(name="sb", bufs=1))
        ps = ctx.enter_context(tc.psum_pool(name="ps", bufs=1))
        ctx.enter_context(tc.manual_schedule())

        def tiles(name, count, shape, dtype):
            return [sb.tile(shape, dtype, name="%s%d" % (name, i), align_bytes=ALIGN) for i in range(count)]

        banks = [ps.tile([P, N], F32, name="bank%d" % i) for i in range(BANKS)]
        ident = sb.tile([P, P], F32, name="ident")
        ones = sb.tile([P, PACK * P], BF16, name="ones", align_bytes=ALIGN)
        warm_codes = sb.tile([P, P], U32, name="warm_codes", align_bytes=ALIGN)
        warm_scales = sb.tile([P, P], U8, name="warm_scales", align_bytes=ALIGN)
        junk = sb.tile([P, 8], F32, name="junk")
        m_bf = sb.tile([P, GROUPS, PACK], BF16, name="m_bf")
        m_f32 = sb.tile([P, GROUPS * PACK], F32, name="m_f32")
        m_frac = sb.tile([P, GROUPS * PACK], F32, name="m_frac")
        m_pow = sb.tile([P, GROUPS * PACK], F32, name="m_pow")
        m_log = sb.tile([P, GROUPS * PACK], F32, name="m_log")

        x_raw = [tiles("x_raw%d_" % h, 3, [P, TILES * KP], BF16) for h in range(HALVES)]
        x_stage = tiles("x_stage", PASSES, [P, N * PACK], BF16)
        x_codes = [tiles("x_codes%d_" % h, PASSES, [P, N], U32) for h in range(HALVES)]
        x_scales = [tiles("x_scales%d_" % h, PASSES, [P, N], U8) for h in range(HALVES)]
        f_raw = [sb.tile([P, 2, 2 * KP * (hi - lo)], U8, name="f_raw%d" % lo, align_bytes=ALIGN) for lo, hi in PARTS]
        f_perm = tiles("f_perm", GROUPS, [P, 2, 2 * KP], U8)
        fs_first = sb.tile([P, 2, KP], U8, name="fs_first", align_bytes=ALIGN)
        fs_rest = sb.tile([P, 2, S - KP], U8, name="fs_rest", align_bytes=ALIGN)
        fs_perm = tiles("fs_perm", GROUPS, [P, 2, KP], U8)
        g_raw = [sb.tile([P, PACK, KP * (hi - lo)], BF16, name="g_raw%d" % lo, align_bytes=ALIGN) for lo, hi in PARTS]
        g_stage = tiles("g_stage", 2, [P, KP * PACK], BF16)
        g_codes = tiles("g_codes", GROUPS, [P, KP], U32)
        g_scales = tiles("g_scales", GROUPS, [P, KP], U8)
        a_sb = sb.tile([P, GROUPS, 2 * E], U8, name="a_sb", align_bytes=ALIGN)
        as_sb = sb.tile([P, GROUPS, E], U8, name="as_sb", align_bytes=ALIGN)
        feed_sb = tiles("feed_sb", HALVES, [P, TILES, E], BF16)
        n_rows = [tiles("n_rows%d_" % G, HALVES, [P, PACK, N], BF16) for G in range(GROUPS)]
        n_stage = tiles("n_stage", 3, [P, N * PACK], BF16)
        n_codes = [tiles("n_codes%d_" % G, HALVES, [P, N], U32) for G in range(GROUPS)]
        n_scales = [tiles("n_scales%d_" % G, HALVES, [P, N], U8) for G in range(GROUPS)]
        res = tiles("res", BANKS, [P, N], F32)

        vector_copy = nc.vector.tensor_copy
        scalar_copy = nc.scalar.copy

        def cells(src, h):
            return src[h * N:(h + 1) * N, :].rearrange("(p b) k -> p b k", b=TILES)

        def load_x(h, j):
            src = cells(phi, h) if j == PHI else cells(lam, h)[:, 2 * j:2 * j + 2, :]
            nc.sync.dma_start(out=x_raw[h][j][:], in_=src.rearrange("p b k -> p (b k)"))

        def load_scale_rows(dst, src):
            for r in range(4):
                nc.sync.dma_start(out=dst[:].bitcast(I32)[r:P:32, :, :],
                                  in_=src[:, r:16:4, :].rearrange("c q n -> q c n").bitcast(I32))

        def load_f(part):
            lo, hi = PARTS[part]
            src = f_words[:, :, lo * 2 * KP:hi * 2 * KP]
            nc.sync.dma_start(out=f_raw[part][:].bitcast(I32), in_=src.rearrange("c p n -> p c n").bitcast(I32))

        def load_g(part):
            lo, hi = PARTS[part]
            nc.sync.dma_start(out=g_raw[part][:], in_=g[:, lo * KP:hi * KP].rearrange("(p j) s -> p j s", j=PACK))

        load_x(0, 0)
        load_x(0, 1)
        load_f(0)
        nc.scalar.dma_start(out=m_bf[:], in_=m.rearrange("(G p t) -> p G t", p=P, t=PACK))
        nc.gpsimd.memset(ones[:], 1.0)
        nc.vector.memset(fs_first[:].bitcast(I32), 0)
        nc.vector.quantize_mx(out=warm_codes[:].bitcast(FP8X4), scales=warm_scales[:], in_=ones[:])
        load_scale_rows(fs_first, f_scales[:, :, 0:KP])
        nc.scalar.activation(out=junk[:, 0:1], in_=ones[:, 0:1], func=ACT.Ln)
        make_identity(nc, ident[:])
        nc.vector.memset(fs_rest[:].bitcast(I32), 0)
        nc.vector.memset(as_sb[:].bitcast(I32), 0)

        load_x(0, PHI)
        load_x(1, 0)
        load_g(0)
        load_x(1, 1)
        load_x(1, PHI)
        load_scale_rows(fs_rest, f_scales[:, :, KP:S])
        for part in (1, 2):
            load_f(part)
            load_g(part)
        load_scale_rows(as_sb, a_scales)
        nc.sync.dma_start(out=a_sb[:].bitcast(I32), in_=a_words.rearrange("c p n -> p c n").bitcast(I32))
        for h in range(HALVES):
            nc.sync.dma_start(out=feed_sb[h][:], in_=cells(feed, h))

        mantissa_bits, bits_of_one, mantissa_width = 0x007FFFFF, 0x3F800000, 23
        nc.vector.tensor_copy(out=m_f32[:], in_=m_bf[:].rearrange("p G t -> p (G t)"))
        nc.vector.tensor_scalar(out=m_frac[:].bitcast(I32), in0=m_f32[:].bitcast(I32), scalar1=mantissa_bits,
                                scalar2=bits_of_one, op0=ALU.bitwise_and, op1=ALU.bitwise_or)
        nc.vector.tensor_scalar(out=m_pow[:].bitcast(I32), in0=m_f32[:].bitcast(I32), scalar1=mantissa_width,
                                scalar2=mantissa_width, op0=ALU.logical_shift_right, op1=ALU.logical_shift_left)
        nc.scalar.activation(out=m_log[:], in_=m_frac[:], func=ACT.Ln)
        nc.scalar.activation(out=junk[:, 1:2], in_=ones[:, 0:1], func=ACT.Exp)

        def warm(count):
            for i in range(count):
                col = (i % PACK) * P
                nc.tensor.matmul_mx(out=banks[0][:, col:col + P], lhsT=warm_codes[:].bitcast(FP8X4), lhsT_scale=warm_scales[:],
                                    rhs=warm_codes[:].bitcast(FP8X4), rhs_scale=warm_scales[:], start=True, stop=True)

        def transpose_pairs(pairs_of, j, first_bank):
            for y in range(2):
                runs = (2 * y, 2 * y + 1) if j == PHI else (y, 2 + y)
                for b, q in enumerate(runs):
                    for u in range(2):
                        col = (2 * b + u) * P
                        nc.tensor.transpose(banks[first_bank + y][:, col:col + P], pairs_of(q, u), ident[:])

        def transpose_stepped(h, j, first_bank):
            pairs = x_raw[h][j][:].bitcast(F32).rearrange("p (q w) -> p q w", q=4)
            transpose_pairs(lambda q, u: pairs[:, q, u:2 * P:2], j, first_bank)

        def split_pairs(j, copy):
            copy(out=n_stage[j][:].bitcast(F32).rearrange("p (q u i) -> p q u i", q=4, u=2),
                 in_=x_raw[1][j][:].bitcast(F32).rearrange("p (q i u) -> p q u i", q=4, u=2))

        def transpose_split(j, first_bank):
            pairs = n_stage[j][:].bitcast(F32).rearrange("p (q u i) -> p q u i", q=4, u=2)
            transpose_pairs(lambda q, u: pairs[:, q, u, :], j, first_bank)

        def evacuate_x(j, first_bank, y, copy):
            c, tile_pair = (PHI, y) if j == PHI else (y, j)
            stage = x_stage[c][:].bitcast(F32)
            copy(out=stage[:, tile_pair * N:(tile_pair + 1) * N].rearrange("p (b r u) -> p b r u", b=2, u=2),
                 in_=banks[first_bank + y][:].rearrange("p (b u r) -> p b r u", b=2, u=2))

        def quantize(codes, scales, stage, lo=0, hi=N):
            nc.vector.quantize_mx(out=codes[:, lo:hi].bitcast(FP8X4), scales=scales[:, lo:hi], in_=stage[:, PACK * lo:PACK * hi])

        def quantize_x(h, c):
            quantize(x_codes[h][c], x_scales[h][c], x_stage[c])

        def part_of(G):
            part = min(G, len(PARTS) - 1)
            return part, G - PARTS[part][0]

        def permute_words(G, c):
            part, at = part_of(G)
            src = f_raw[part][:, c, at * 2 * KP:(at + 1) * 2 * KP]
            nc.vector.tensor_copy(out=f_perm[G][:, c, :].rearrange("p (t i y) -> p t i y", t=PACK, y=2),
                                  in_=src.rearrange("p (i t y) -> p t i y", t=PACK, y=2))

        def permute_scales(G, c):
            src = fs_first[:, c, :] if G == 0 else fs_rest[:, c, (G - 1) * KP:G * KP]
            nc.vector.tensor_copy(out=fs_perm[G][:, c, :].rearrange("p (t i) -> p t i", t=PACK),
                                  in_=src.rearrange("p (i t) -> p t i", t=PACK))

        def permute_f(G, c):
            permute_words(G, c)
            permute_scales(G, c)

        def interleave_g(G, copy):
            part, at = part_of(G)
            copy(out=g_stage[G % 2][:].rearrange("p (t i j) -> p i t j", t=PACK, j=PACK),
                 in_=g_raw[part][:, :, at * KP:(at + 1) * KP].rearrange("p j (i t) -> p i t j", t=PACK))

        def quantize_g(G):
            quantize(g_codes[G], g_scales[G], g_stage[G % 2])

        def z_pass(G, h, t, c, bank):
            if c == PHI:
                lhsT = g_codes[G][:, P * t:P * (t + 1)].bitcast(FP8X4)
                lhsT_scale = g_scales[G][:, P * t:P * (t + 1)]
            else:
                lhsT = f_perm[G][:, c, 2 * P * t:2 * P * (t + 1)].bitcast(FP4X4)
                lhsT_scale = fs_perm[G][:, c, P * t:P * (t + 1)]
            nc.tensor.matmul_mx(out=banks[bank][:], lhsT=lhsT, lhsT_scale=lhsT_scale, rhs=x_codes[h][c][:].bitcast(FP8X4),
                                rhs_scale=x_scales[h][c][:], start=(c == 0), stop=(c == PASSES - 1))

        def exp_z(G, h, t, bank):
            col = PACK * G + t
            nc.scalar.activation(out=n_rows[G][h][:, t, :], in_=banks[bank][:], func=ACT.Exp, bias=m_log[:, col:col + 1])

        def pass_of_all_t(G, h, c, bank_set):
            for t in range(PACK):
                z_pass(G, h, t, c, bank_set[t])

        def exp_of_all_t(G, h, bank_set):
            for t in range(PACK):
                exp_z(G, h, t, bank_set[t])

        def z_by_pass(G, h):
            for c in range(PASSES):
                pass_of_all_t(G, h, c, Z_BANKS[h])
            exp_of_all_t(G, h, Z_BANKS[h])

        def z_by_bank(G, h):
            for t in range(PACK):
                for c in range(PASSES):
                    z_pass(G, h, t, c, Z_BANKS[h][t])
                exp_z(G, h, t, Z_BANKS[h][t])

        def scale_n(G, h):
            for t in range(PACK):
                col = PACK * G + t
                nc.vector.tensor_scalar(out=n_rows[G][h][:, t, :], in0=n_rows[G][h][:, t, :], scalar1=m_pow[:, col:col + 1],
                                        scalar2=None, op0=ALU.mult)

        def interleave_n(G, h, slot, copy, lo=0, hi=N):
            copy(out=n_stage[slot][:, PACK * lo:PACK * hi].rearrange("p (b t) -> p b t", t=PACK),
                 in_=n_rows[G][h][:, :, lo:hi].rearrange("p t b -> p b t"))

        def quantize_n(G, h, slot, lo=0, hi=N):
            quantize(n_codes[G][h], n_scales[G][h], n_stage[slot], lo, hi)

        def balance(i, bank, lo, hi, queue):
            cell_tile, e_half = divmod(i, 2)
            h, b = divmod(cell_tile, TILES)
            cols = slice(N * e_half + lo, N * e_half + hi)
            for G in range(GROUPS):
                nc.tensor.matmul_mx(out=banks[bank][:, lo:hi], lhsT=n_codes[G][h][:, P * b:P * (b + 1)].bitcast(FP8X4),
                                    lhsT_scale=n_scales[G][h][:, P * b:P * (b + 1)],
                                    rhs=a_sb[:, G, 2 * cols.start:2 * cols.stop].bitcast(FP4X4),
                                    rhs_scale=as_sb[:, G, cols], start=(G == 0), stop=(G == GROUPS - 1))
            result = res[i % BANKS]
            nc.vector.tensor_tensor(out=result[:, lo:hi], in0=banks[bank][:, lo:hi], in1=feed_sb[h][:, b, cols], op=ALU.subtract)
            queue.dma_start(out=cells(out, h)[:, b, cols], in_=result[:, lo:hi])


        warm(WARM_AT_START)
        transpose_stepped(0, 0, 4)
        transpose_stepped(0, 1, 6)
        evacuate_x(0, 4, 0, vector_copy)
        evacuate_x(0, 4, 1, scalar_copy)
        evacuate_x(1, 6, 0, vector_copy)
        evacuate_x(1, 6, 1, scalar_copy)
        permute_words(0, 0)
        quantize_x(0, 0)
        permute_scales(0, 0)
        warm(WARM_BEFORE_PHI)
        transpose_stepped(0, PHI, 4)
        evacuate_x(PHI, 4, 0, scalar_copy)
        evacuate_x(PHI, 4, 1, scalar_copy)
        permute_f(0, 1)
        quantize_x(0, 1)
        pass_of_all_t(0, 0, 0, FIRST_BANKS)
        pass_of_all_t(0, 0, 1, FIRST_BANKS)

        split_pairs(0, scalar_copy)
        quantize_x(0, PHI)
        interleave_g(0, vector_copy)
        quantize_g(0)
        transpose_split(0, 6)
        transpose_stepped(1, 1, 4)
        pass_of_all_t(0, 0, PHI, FIRST_BANKS)
        split_pairs(PHI, vector_copy)
        for y in range(2):
            evacuate_x(0, 6, y, scalar_copy)
            evacuate_x(1, 4, y, scalar_copy)
        transpose_split(PHI, 6)
        exp_of_all_t(0, 0, FIRST_BANKS)
        quantize_x(1, 0)
        permute_words(1, 0)
        quantize_x(1, 1)
        evacuate_x(PHI, 6, 0, vector_copy)
        evacuate_x(PHI, 6, 1, vector_copy)
        permute_scales(1, 0)
        quantize_x(1, PHI)
        z_by_pass(0, 1)

        permute_f(1, 1)
        interleave_g(1, vector_copy)
        permute_scales(2, 0)
        quantize_g(1)
        interleave_g(2, scalar_copy)
        z_by_pass(1, 0)
        scale_n(0, 0)
        permute_words(2, 0)
        interleave_n(0, 0, 0, vector_copy)
        permute_f(2, 1)
        quantize_g(2)
        quantize_n(0, 0, 0)
        z_by_bank(1, 1)
        z_by_bank(2, 0)
        scale_n(1, 0)
        permute_f(3, 0)
        interleave_g(3, vector_copy)
        permute_f(3, 1)
        quantize_g(3)
        interleave_n(1, 0, 2, vector_copy)
        scale_n(2, 0)
        quantize_n(1, 0, 2)
        z_by_bank(2, 1)
        z_by_bank(3, 0)
        interleave_n(2, 0, 0, vector_copy)
        scale_n(0, 1)
        quantize_n(2, 0, 0)
        scale_n(1, 1)
        interleave_n(0, 1, 1, scalar_copy)
        z_by_bank(3, 1)
        scale_n(3, 0)
        pieces = [(0, N // 2), (N // 2, N)]
        for lo, hi in pieces:
            interleave_n(3, 0, 2, vector_copy, lo, hi)
        for lo, hi in pieces:
            quantize_n(3, 0, 2, lo, hi)
        scale_n(2, 1)
        quantize_n(0, 1, 1)
        interleave_n(1, 1, 0, scalar_copy)
        interleave_n(2, 1, 1, scalar_copy)

        ring = Z_BANKS[0] + Z_BANKS[1]
        after_block = {
            0: [lambda: scale_n(3, 1)],
            1: [lambda: interleave_n(3, 1, 2, vector_copy)],
            2: [lambda: quantize_n(1, 1, 0), lambda: quantize_n(3, 1, 2)],
            4: [lambda: quantize_n(2, 1, 1)],
        }
        last = 2 * HALVES * TILES - 1
        for i in range(last):
            balance(i, ring[i % BANKS], 0, N, nc.sync)
            for step in after_block.get(i, []):
                step()
        for q in range(N // P):
            balance(last, ring[(last + q) % BANKS], q * P, (q + 1) * P, nc.scalar if q % 2 == 0 else nc.sync)
